import numpy as np
import ml_dtypes


def mxq(x, axis, fmt="e4m3"):
    dtype, down = {"e4m3": (ml_dtypes.float8_e4m3fn, 7), "e5m2": (ml_dtypes.float8_e5m2, 14)}[fmt]
    v = np.moveaxis(np.asarray(x, np.float32).astype(ml_dtypes.bfloat16).astype(np.float64), axis, -1)
    blocks = v.reshape(v.shape[:-1] + (-1, 32))
    amax = np.abs(blocks).max(-1, keepdims=True)
    byte = np.maximum(np.where(amax > 0, np.frexp(amax)[1] - 1 + 127, 0) - down, 1)
    scale = np.exp2(byte - 127.0)
    codes = (blocks / scale).astype(np.float32).astype(dtype).astype(np.float64)
    return np.moveaxis((codes * scale).reshape(v.shape), -1, axis)


WIDE = False


def mx_kscale(k):
    if not WIDE:
        return np.ones(k)
    levels = np.array([10, -10, 5, -5, 0])
    if k % 512:
        return np.exp2(np.random.permutation(np.resize(levels, k // 32))).repeat(32)
    a = np.empty((k // 512, 16))
    for p in range(k // 512):
        a[p, :8] = np.random.permutation(np.resize(levels, 8))
        for g in range(8):
            far = levels[np.abs(levels - a[p, g]) >= 10]
            a[p, g + 8] = far[np.random.randint(len(far))]
    return np.exp2(a.ravel()).repeat(32)


def f64(x):
    return np.asarray(x).astype(np.float64)


def striped(idx):
    return np.tile(np.asarray(idx).reshape(-1, 16).T, (8, 1)).astype(np.uint16)


def unstriped(offs):
    return offs[:16].T.reshape(-1).astype(np.int64)


E2M1 = np.array([0.0, 0.5, 1.0, 1.5, 2.0, 3.0, 4.0, 6.0, -0.0, -0.5, -1.0, -1.5, -2.0, -3.0, -4.0, -6.0])


def pack_weight(w, fmt):
    k, n = w.shape
    w = f64(np.asarray(w, np.float32).astype(ml_dtypes.bfloat16)).reshape(k // 32, 32, n)
    amax = np.abs(w).max(1)
    if fmt == "e4m3":
        byte = np.frexp(amax)[1] - 1 + 127 - 7
    else:
        mant, ex = np.frexp(amax / 6.0)
        byte = np.where(mant > 0.5, ex, ex - 1) + 127
    byte = np.clip(np.where(amax > 0, byte, 1), 1, 254)
    scaled = (w * np.exp2(127.0 - byte)[:, None, :]).reshape(k, n).astype(np.float32)
    by_word = np.ascontiguousarray(scaled.reshape(k // 512, 128, 4, n).transpose(0, 1, 3, 2))
    if fmt == "e4m3":
        words = by_word.astype(ml_dtypes.float8_e4m3fn).view(np.uint8)
    else:
        c = by_word.astype(ml_dtypes.float4_e2m1fn).view(np.uint8) & 0xF
        words = (c[..., 0::2] | (c[..., 1::2] << 4)).reshape(k // 512, 128, 2 * n)
    return np.ascontiguousarray(words), np.ascontiguousarray(byte.astype(np.uint8).reshape(k // 512, 16, n))


def unpack_weight(words, scales, fmt):
    g, _, n = scales.shape
    words = np.ascontiguousarray(words).reshape(g, 128, n, -1)
    if fmt == "e4m3":
        vals = words.view(ml_dtypes.float8_e4m3fn).astype(np.float64)
    else:
        nib = np.empty((g, 128, n, 4), np.uint8)
        nib[..., 0::2] = words & 0xF
        nib[..., 1::2] = words >> 4
        vals = E2M1[nib]
    vals = vals * np.repeat(np.exp2(scales.astype(np.float64) - 127.0), 8, axis=1)[..., None]
    return vals.transpose(0, 1, 3, 2).reshape(g * 512, n)


D, K, T, I, U, Q = 512, 1024, 4096, 1024, 512, 128


def setup_inputs():
    n = np.random.standard_normal
    idx = np.random.permutation(T)[:I]
    idx2 = np.random.randint(0, U, I)
    fd = mx_kscale(D)
    fk = mx_kscale(K)
    tailp = pack_weight(n((K, T)) / fk[:, None], "e2m1")
    return {
        "hid": (n((D, Q)) * 1.0 / np.sqrt(D) * fd[:, None]).astype(np.float32),
        "head": (n((D, U)) / fd[:, None]).astype(np.float32),
        "tl": (np.random.uniform(0.5, 1.5, (Q, U))).astype(np.float32),
        "htail": (n((K, Q)) * 1.0 / np.sqrt(K) * fk[:, None]).astype(np.float32),
        "tail_words": tailp[0],
        "tail_scales": tailp[1],
        "offs": striped(idx),
        "offs2": striped(idx2),
    }


def reference(hid, head, tl, htail, tail_words, tail_scales, offs, offs2):
    idx = unstriped(offs)
    idx2 = unstriped(offs2)
    tailu = unpack_weight(tail_words, tail_scales, "e2m1")
    hidq = mxq(f64(hid), 0, "e4m3")
    headq = mxq(f64(head), 0, "e4m3")
    a = hidq.T @ headq
    p = np.exp(a)
    b = a - np.log(np.sum(p, axis=1, keepdims=True)) - f64(tl)
    htailq = mxq(f64(htail), 0, "e4m3")
    tailidxg = tailu[:, idx]
    r = htailq.T @ tailidxg
    y = b[:, idx2] + r
    return y

@@ -1,0 +1,159 @@
+from contextlib import ExitStack
+
+import concourse.mybir as mybir
+
+D, K, T, I, U, Q = 512, 1024, 4096, 1024, 512, 128
+FLOPS = 2 * Q * D * U + 2 * Q * K * I
+
+F32 = mybir.dt.float32
+BF16 = mybir.dt.bfloat16
+I32 = mybir.dt.int32
+U32 = mybir.dt.uint32
+U16 = mybir.dt.uint16
+U8 = mybir.dt.uint8
+FP8X4 = mybir.dt.float8_e4m3fn_x4
+FP4X4 = mybir.dt.float4_e2m1fn_x4
+ALU = mybir.AluOpType
+ACT = mybir.ActivationFunctionType
+
+P = 128
+PACK = 4
+PASSES = K // (P * PACK)
+BANK = 512
+LIST_COLS = I // 16
+SPARE = 32
+
+
+def interleave(copy, grouped, raw):
+    copy(
+        out=grouped.rearrange("p (c i) t -> p c t i", i=4),
+        in_=raw.rearrange("p t (c i) -> p c t i", i=4),
+    )
+
+
+def quantise(nc, codes, scales, grouped):
+    nc.vector.quantize_mx(out=codes.bitcast(FP8X4), scales=scales, in_=grouped.rearrange("p c t -> p (c t)"))
+
+
+def tile_attend_adaptivesoftmax_kernel(tc, hid, head, tl, htail, tail_words, tail_scales, offs, offs2, out):
+    nc = tc.nc
+    with ExitStack() as ctx:
+        sb = ctx.enter_context(tc.tile_pool(name="sb", bufs=1))
+        ps = ctx.enter_context(tc.psum_pool(name="ps", bufs=1))
+
+        word_list = sb.tile([P, LIST_COLS], U16, name="word_list")
+        cluster_list = sb.tile([P, LIST_COLS], U16, name="cluster_list")
+        scale_rows = sb.tile([P, T], U8, name="scale_rows", align_bytes=64)
+        words = [sb.tile([P, T], U16, name=f"words{z}", align_bytes=64) for z in range(PASSES)]
+        half = U // 2
+        head_raw = [sb.tile([P, PACK, half], F32, name=f"head_raw{h}") for h in range(2)]
+        hid_raw = sb.tile([P, PACK, Q], F32, name="hid_raw")
+        htail_raw = sb.tile([P, PASSES, PACK, Q], F32, name="htail_raw")
+        tl_sb = sb.tile([P, U], F32, name="tl_sb")
+        b = sb.tile([P, U + SPARE], F32, name="b")
+        tail_planes = [sb.tile([P, I], U8, name=f"tail_plane{z}", align_bytes=64) for z in range(PASSES)]
+
+        nc.vector.memset(scale_rows[0:96, :].bitcast(I32), 0)
+        nc.sync.dma_start(
+            out=scale_rows[96:P, :].bitcast(I32),
+            in_=tail_scales.rearrange("z f t -> (z f) t").bitcast(I32),
+        )
+        nc.vector.memset(b[:, U:], 0.0)
+        for z in range(PASSES):
+            nc.vector.memset(tail_planes[z][:].bitcast(I32), 0)
+
+        head_k = head.rearrange("(p t) u -> p t u", t=PACK)
+        nc.sync.dma_start(word_list[:], offs)
+        nc.sync.dma_start(out=head_raw[0][:], in_=head_k[:, :, 0:half])
+        nc.sync.dma_start(out=hid_raw[:], in_=hid.rearrange("(p t) q -> p t q", t=PACK))
+        nc.sync.dma_start(out=head_raw[1][:], in_=head_k[:, :, half:U])
+        nc.sync.dma_start(out=words[0][:].bitcast(I32), in_=tail_words[0].bitcast(I32))
+        nc.sync.dma_start(out=words[1][:].bitcast(I32), in_=tail_words[1].bitcast(I32))
+        nc.sync.dma_start(out=htail_raw[:], in_=htail.rearrange("(z p t) q -> p z t q", p=P, t=PACK))
+        nc.sync.dma_start(cluster_list[:], offs2)
+        nc.sync.dma_start(out=tl_sb[:], in_=tl)
+
+        picked_scales = sb.tile([P, I], U8, name="picked_scales", align_bytes=64)
+        nc.vector.tensor_copy(picked_scales[:], scale_rows[:].indirect(word_list[:]))
+        for z in range(PASSES):
+            for quad in range(4):
+                first = 96 + 16 * z + 4 * quad
+                nc.sync.dma_start(
+                    out=tail_planes[z][32 * quad : 32 * quad + 4, :].bitcast(I32),
+                    in_=picked_scales[first : first + 4, :].bitcast(I32),
+                )
+
+        quarter = U // 4
+        head_g0 = sb.tile([P, half, PACK], BF16, name="head_g0", align_bytes=64)
+        head_g2 = sb.tile([P, quarter, PACK], BF16, name="head_g2", align_bytes=64)
+        head_g3 = sb.tile([P, quarter, PACK], BF16, name="head_g3", align_bytes=64)
+        hid_g = sb.tile([P, Q, PACK], BF16, name="hid_g", align_bytes=64)
+        head_codes = sb.tile([P, U], U32, name="head_codes", tag="reused", align_bytes=64)
+        head_plane = sb.tile([P, U], U8, name="head_plane", align_bytes=64)
+        hid_codes = sb.tile([P, Q], U32, name="hid_codes", align_bytes=64)
+        hid_plane = sb.tile([P, Q], U8, name="hid_plane", align_bytes=64)
+        interleave(nc.scalar.copy, head_g0[:], head_raw[0][:])
+        interleave(nc.scalar.copy, hid_g[:], hid_raw[:])
+        interleave(nc.scalar.copy, head_g2[:], head_raw[1][:, :, 0:quarter])
+        interleave(nc.vector.tensor_copy, head_g3[:], head_raw[1][:, :, quarter:half])
+        quantise(nc, head_codes[:, 0:half], head_plane[:, 0:half], head_g0[:])
+        quantise(nc, hid_codes[:], hid_plane[:], hid_g[:])
+        quantise(nc, head_codes[:, half + quarter : U], head_plane[:, half + quarter : U], head_g3[:])
+        quantise(nc, head_codes[:, half : half + quarter], head_plane[:, half : half + quarter], head_g2[:])
+        a = ps.tile([P, U], F32, name="a")
+        nc.tensor.matmul_mx(
+            out=a[:], lhsT=hid_codes[:].bitcast(FP8X4), lhsT_scale=hid_plane[:],
+            rhs=head_codes[:].bitcast(FP8X4), rhs_scale=head_plane[:], start=True, stop=True,
+        )
+        neg_max = sb.tile([P, 1], F32, name="neg_max")
+        nc.vector.tensor_reduce(out=neg_max[:], in_=a[:], axis=mybir.AxisListType.X, op=ALU.max, negate=True)
+        exps = sb.tile([P, U], F32, name="exps")
+        row_sum = sb.tile([P, 1], F32, name="row_sum")
+        nc.scalar.activation(out=exps[:], in_=a[:], func=ACT.Exp, bias=neg_max[:], accum_out=row_sum[:])
+        log_sum = sb.tile([P, 1], F32, name="log_sum")
+        nc.scalar.activation(out=log_sum[:], in_=row_sum[:], func=ACT.Ln)
+        neg_lse = sb.tile([P, 1], F32, name="neg_lse")
+        nc.scalar.activation(out=neg_lse[:], in_=log_sum[:], func=ACT.Identity, scale=-1.0, bias=neg_max[:])
+
+        picked_words = {}
+        for z in range(PASSES):
+            for h in range(I // BANK):
+                tag = "reused" if (z, h) == (0, 1) else f"picked_words{z}{h}"
+                picked_words[z, h] = sb.tile([P, BANK], U16, name=f"picked_words{z}{h}", tag=tag, align_bytes=64)
+                nc.vector.tensor_copy(
+                    picked_words[z, h][:], words[z][:].indirect(word_list[:, h * BANK // 16 : (h + 1) * BANK // 16])
+                )
+
+        htail_g = sb.tile([P, PASSES * Q, PACK], BF16, name="htail_g", align_bytes=64)
+        for z in range(PASSES):
+            interleave(nc.scalar.copy, htail_g[:, z * Q : (z + 1) * Q, :], htail_raw[:, z, :, :])
+        htail_codes = sb.tile([P, PASSES * Q], U32, name="htail_codes", align_bytes=64)
+        htail_plane = sb.tile([P, PASSES * Q], U8, name="htail_plane", align_bytes=64)
+
+        for z in range(PASSES):
+            qs = slice(z * Q, (z + 1) * Q)
+            quantise(nc, htail_codes[:, qs], htail_plane[:, qs], htail_g[:, qs, :])
+        nc.vector.scalar_tensor_tensor(
+            out=b[:, 0:U], in0=a[:], scalar=neg_lse[:], in1=tl_sb[:], op0=ALU.add, op1=ALU.subtract
+        )
+
+        for h in range(I // BANK):
+            cols = slice(h * BANK, (h + 1) * BANK)
+            r = ps.tile([P, BANK], F32, name=f"r{h}")
+            for z in range(PASSES):
+                nc.tensor.matmul_mx(
+                    out=r[:],
+                    lhsT=htail_codes[:, z * Q : (z + 1) * Q].bitcast(FP8X4),
+                    lhsT_scale=htail_plane[:, z * Q : (z + 1) * Q],
+                    rhs=picked_words[z, h][:].bitcast(FP4X4),
+                    rhs_scale=tail_planes[z][:, cols],
+                    start=(z == 0),
+                    stop=(z == PASSES - 1),
+                )
+            picked_b = sb.tile([P, BANK], F32, name=f"picked_b{h}")
+            nc.vector.tensor_copy(
+                picked_b[:], b[:].indirect(cluster_list[:, h * BANK // 16 : (h + 1) * BANK // 16])
+            )
+            result = sb.tile([P, BANK], F32, name=f"result{h}")
+            nc.vector.tensor_tensor(out=result[:], in0=r[:], in1=picked_b[:], op=ALU.add)
+            nc.sync.dma_start(out=out[:, cols], in_=result[:])

@@ -22,6 +22,7 @@ PASSES = K // (P * PACK)
 BANK = 512
 LIST_COLS = I // 16
 SPARE = 32
+PIECES = ((0, 512), (512, 896), (896, 1024))
 
 
 def interleave(copy, grouped, raw):
@@ -43,13 +44,12 @@ def tile_attend_adaptivesoftmax_kernel(tc, hid, head, tl, htail, tail_words, tai
 
         word_list = sb.tile([P, LIST_COLS], U16, name="word_list")
         cluster_list = sb.tile([P, LIST_COLS], U16, name="cluster_list")
-        scale_rows = sb.tile([P, T], U8, name="scale_rows", align_bytes=64)
-        words = [sb.tile([P, T], U16, name=f"words{z}", align_bytes=64) for z in range(PASSES)]
-        half = U // 2
-        head_raw = [sb.tile([P, PACK, half], F32, name=f"head_raw{h}") for h in range(2)]
-        hid_raw = sb.tile([P, PACK, Q], F32, name="hid_raw")
+        scale_rows = sb.tile([P, T], U8, name="scale_rows", tag="rows_then_words", align_bytes=64)
+        first_words = sb.tile([P, T], U16, name="first_words", align_bytes=64)
         htail_raw = sb.tile([P, PASSES, PACK, Q], F32, name="htail_raw")
-        tl_sb = sb.tile([P, U], F32, name="tl_sb")
+        half = U // 2
+        head_raw = sb.tile([P, PACK, U], F32, name="head_raw", tag="head_then_tl")
+        hid_raw = sb.tile([P, PACK, Q], F32, name="hid_raw")
         b = sb.tile([P, U + SPARE], F32, name="b")
         tail_planes = [sb.tile([P, I], U8, name=f"tail_plane{z}", align_bytes=64) for z in range(PASSES)]
 
@@ -62,20 +62,17 @@ def tile_attend_adaptivesoftmax_kernel(tc, hid, head, tl, htail, tail_words, tai
         for z in range(PASSES):
             nc.vector.memset(tail_planes[z][:].bitcast(I32), 0)
 
-        head_k = head.rearrange("(p t) u -> p t u", t=PACK)
         nc.sync.dma_start(word_list[:], offs)
-        nc.sync.dma_start(out=head_raw[0][:], in_=head_k[:, :, 0:half])
         nc.sync.dma_start(out=hid_raw[:], in_=hid.rearrange("(p t) q -> p t q", t=PACK))
-        nc.sync.dma_start(out=head_raw[1][:], in_=head_k[:, :, half:U])
-        nc.sync.dma_start(out=words[0][:].bitcast(I32), in_=tail_words[0].bitcast(I32))
-        nc.sync.dma_start(out=words[1][:].bitcast(I32), in_=tail_words[1].bitcast(I32))
+        nc.sync.dma_start(out=head_raw[:], in_=head.rearrange("(p t) u -> p t u", t=PACK))
         nc.sync.dma_start(out=htail_raw[:], in_=htail.rearrange("(z p t) q -> p z t q", p=P, t=PACK))
+        nc.sync.dma_start(out=first_words[:].bitcast(I32), in_=tail_words[0].bitcast(I32))
         nc.sync.dma_start(cluster_list[:], offs2)
-        nc.sync.dma_start(out=tl_sb[:], in_=tl)
 
         picked_scales = sb.tile([P, I], U8, name="picked_scales", align_bytes=64)
         nc.vector.tensor_copy(picked_scales[:], scale_rows[:].indirect(word_list[:]))
-        for z in range(PASSES):
+
+        def place_scale_rows(z):
             for quad in range(4):
                 first = 96 + 16 * z + 4 * quad
                 nc.sync.dma_start(
@@ -83,28 +80,31 @@ def tile_attend_adaptivesoftmax_kernel(tc, hid, head, tl, htail, tail_words, tai
                     in_=picked_scales[first : first + 4, :].bitcast(I32),
                 )
 
-        quarter = U // 4
-        head_g0 = sb.tile([P, half, PACK], BF16, name="head_g0", align_bytes=64)
-        head_g2 = sb.tile([P, quarter, PACK], BF16, name="head_g2", align_bytes=64)
-        head_g3 = sb.tile([P, quarter, PACK], BF16, name="head_g3", align_bytes=64)
+        place_scale_rows(0)
+        second_words = sb.tile([P, T], U16, name="second_words", tag="rows_then_words", align_bytes=64)
+        nc.sync.dma_start(out=second_words[:].bitcast(I32), in_=tail_words[1].bitcast(I32))
+        place_scale_rows(1)
+
+        head_g = [sb.tile([P, half, PACK], BF16, name=f"head_g{h}", align_bytes=64) for h in range(2)]
         hid_g = sb.tile([P, Q, PACK], BF16, name="hid_g", align_bytes=64)
-        head_codes = sb.tile([P, U], U32, name="head_codes", tag="reused", align_bytes=64)
+        head_codes = sb.tile([P, U], U32, name="head_codes", tag="codes_then_words", align_bytes=64)
         head_plane = sb.tile([P, U], U8, name="head_plane", align_bytes=64)
         hid_codes = sb.tile([P, Q], U32, name="hid_codes", align_bytes=64)
         hid_plane = sb.tile([P, Q], U8, name="hid_plane", align_bytes=64)
-        interleave(nc.scalar.copy, head_g0[:], head_raw[0][:])
         interleave(nc.scalar.copy, hid_g[:], hid_raw[:])
-        interleave(nc.scalar.copy, head_g2[:], head_raw[1][:, :, 0:quarter])
-        interleave(nc.vector.tensor_copy, head_g3[:], head_raw[1][:, :, quarter:half])
-        quantise(nc, head_codes[:, 0:half], head_plane[:, 0:half], head_g0[:])
+        interleave(nc.vector.tensor_copy, head_g[0][:], head_raw[:, :, 0:half])
+        interleave(nc.scalar.copy, head_g[1][:], head_raw[:, :, half:U])
+        tl_sb = sb.tile([P, U], F32, name="tl_sb", tag="head_then_tl")
+        nc.sync.dma_start(out=tl_sb[:], in_=tl)
         quantise(nc, hid_codes[:], hid_plane[:], hid_g[:])
-        quantise(nc, head_codes[:, half + quarter : U], head_plane[:, half + quarter : U], head_g3[:])
-        quantise(nc, head_codes[:, half : half + quarter], head_plane[:, half : half + quarter], head_g2[:])
         a = ps.tile([P, U], F32, name="a")
-        nc.tensor.matmul_mx(
-            out=a[:], lhsT=hid_codes[:].bitcast(FP8X4), lhsT_scale=hid_plane[:],
-            rhs=head_codes[:].bitcast(FP8X4), rhs_scale=head_plane[:], start=True, stop=True,
-        )
+        for h in range(2):
+            us = slice(h * half, (h + 1) * half)
+            quantise(nc, head_codes[:, us], head_plane[:, us], head_g[h][:])
+            nc.tensor.matmul_mx(
+                out=a[:, us], lhsT=hid_codes[:].bitcast(FP8X4), lhsT_scale=hid_plane[:],
+                rhs=head_codes[:, us].bitcast(FP8X4), rhs_scale=head_plane[:, us], start=True, stop=True,
+            )
         neg_max = sb.tile([P, 1], F32, name="neg_max")
         nc.vector.tensor_reduce(out=neg_max[:], in_=a[:], axis=mybir.AxisListType.X, op=ALU.max, negate=True)
         exps = sb.tile([P, U], F32, name="exps")
@@ -115,45 +115,48 @@ def tile_attend_adaptivesoftmax_kernel(tc, hid, head, tl, htail, tail_words, tai
         neg_lse = sb.tile([P, 1], F32, name="neg_lse")
         nc.scalar.activation(out=neg_lse[:], in_=log_sum[:], func=ACT.Identity, scale=-1.0, bias=neg_max[:])
 
-        picked_words = {}
-        for z in range(PASSES):
-            for h in range(I // BANK):
-                tag = "reused" if (z, h) == (0, 1) else f"picked_words{z}{h}"
-                picked_words[z, h] = sb.tile([P, BANK], U16, name=f"picked_words{z}{h}", tag=tag, align_bytes=64)
-                nc.vector.tensor_copy(
-                    picked_words[z, h][:], words[z][:].indirect(word_list[:, h * BANK // 16 : (h + 1) * BANK // 16])
-                )
-
         htail_g = sb.tile([P, PASSES * Q, PACK], BF16, name="htail_g", align_bytes=64)
-        for z in range(PASSES):
-            interleave(nc.scalar.copy, htail_g[:, z * Q : (z + 1) * Q, :], htail_raw[:, z, :, :])
         htail_codes = sb.tile([P, PASSES * Q], U32, name="htail_codes", align_bytes=64)
         htail_plane = sb.tile([P, PASSES * Q], U8, name="htail_plane", align_bytes=64)
-
         for z in range(PASSES):
             qs = slice(z * Q, (z + 1) * Q)
+            interleave(nc.scalar.copy, htail_g[:, qs, :], htail_raw[:, z, :, :])
             quantise(nc, htail_codes[:, qs], htail_plane[:, qs], htail_g[:, qs, :])
+
+        first_pass = sb.tile([P, I], U16, name="first_pass", tag="codes_then_words", align_bytes=64)
+        nc.vector.tensor_copy(first_pass[:], first_words[:].indirect(word_list[:]))
+        second_pass = [
+            sb.tile([P, BANK], U16, name="second_pass0", align_bytes=64),
+            sb.tile([P, BANK], U16, name="second_pass1", align_bytes=64),
+        ]
+        for h in range(I // BANK):
+            nc.vector.tensor_copy(
+                second_pass[h][:], second_words[:].indirect(word_list[:, h * BANK // 16 : (h + 1) * BANK // 16])
+            )
+
         nc.vector.scalar_tensor_tensor(
             out=b[:, 0:U], in0=a[:], scalar=neg_lse[:], in1=tl_sb[:], op0=ALU.add, op1=ALU.subtract
         )
 
+        r = sb.tile([P, I], F32, name="r")
         for h in range(I // BANK):
             cols = slice(h * BANK, (h + 1) * BANK)
-            r = ps.tile([P, BANK], F32, name=f"r{h}")
+            r_bank = ps.tile([P, BANK], F32, name=f"r_bank{h}")
             for z in range(PASSES):
                 nc.tensor.matmul_mx(
-                    out=r[:],
+                    out=r_bank[:],
                     lhsT=htail_codes[:, z * Q : (z + 1) * Q].bitcast(FP8X4),
                     lhsT_scale=htail_plane[:, z * Q : (z + 1) * Q],
-                    rhs=picked_words[z, h][:].bitcast(FP4X4),
+                    rhs=(first_pass[:, cols], second_pass[h][:])[z].bitcast(FP4X4),
                     rhs_scale=tail_planes[z][:, cols],
                     start=(z == 0),
                     stop=(z == PASSES - 1),
                 )
-            picked_b = sb.tile([P, BANK], F32, name=f"picked_b{h}")
-            nc.vector.tensor_copy(
-                picked_b[:], b[:].indirect(cluster_list[:, h * BANK // 16 : (h + 1) * BANK // 16])
+            nc.scalar.copy(out=r[:, cols], in_=r_bank[:])
+
+        for first, last in PIECES:
+            result = sb.tile([P, last - first], F32, name=f"result{first}")
+            nc.vector.tensor_tensor(
+                result[:], b[:].indirect(cluster_list[:, first // 16 : last // 16]), r[:, first:last], ALU.add
             )
-            result = sb.tile([P, BANK], F32, name=f"result{h}")
-            nc.vector.tensor_tensor(out=result[:], in0=r[:], in1=picked_b[:], op=ALU.add)
-            nc.sync.dma_start(out=out[:, cols], in_=result[:])
+            nc.sync.dma_start(out=out[:, first:last], in_=result[:])

@@ -23,6 +23,7 @@ BANK = 512
 LIST_COLS = I // 16
 SPARE = 32
 PIECES = ((0, 512), (512, 896), (896, 1024))
+STORES = ((0, 512), (512, 896), (896, 1024))
 
 
 def interleave(copy, grouped, raw):
@@ -44,58 +45,54 @@ def tile_attend_adaptivesoftmax_kernel(tc, hid, head, tl, htail, tail_words, tai
 
         word_list = sb.tile([P, LIST_COLS], U16, name="word_list")
         cluster_list = sb.tile([P, LIST_COLS], U16, name="cluster_list")
-        scale_rows = sb.tile([P, T], U8, name="scale_rows", tag="rows_then_words", align_bytes=64)
-        first_words = sb.tile([P, T], U16, name="first_words", align_bytes=64)
+        scale_rows = sb.tile([P, T], U8, name="scale_rows", tag="rows_then_tl", align_bytes=64)
+        words = [sb.tile([P, T], U16, name=f"words{z}", align_bytes=64) for z in range(PASSES)]
         htail_raw = sb.tile([P, PASSES, PACK, Q], F32, name="htail_raw")
         half = U // 2
-        head_raw = sb.tile([P, PACK, U], F32, name="head_raw", tag="head_then_tl")
+        head_raw = sb.tile([P, PACK, U], F32, name="head_raw")
         hid_raw = sb.tile([P, PACK, Q], F32, name="hid_raw")
         b = sb.tile([P, U + SPARE], F32, name="b")
-        tail_planes = [sb.tile([P, I], U8, name=f"tail_plane{z}", align_bytes=64) for z in range(PASSES)]
+        tail_planes = sb.tile([P, PASSES * I], U8, name="tail_planes", align_bytes=64)
 
         nc.vector.memset(scale_rows[0:96, :].bitcast(I32), 0)
         nc.sync.dma_start(
             out=scale_rows[96:P, :].bitcast(I32),
-            in_=tail_scales.rearrange("z f t -> (z f) t").bitcast(I32),
+            in_=tail_scales.bitcast(I32).rearrange("z f t -> f z t"),
         )
+        nc.vector.memset(tail_planes[:].bitcast(I32), 0)
         nc.vector.memset(b[:, U:], 0.0)
-        for z in range(PASSES):
-            nc.vector.memset(tail_planes[z][:].bitcast(I32), 0)
 
         nc.sync.dma_start(word_list[:], offs)
+        nc.sync.dma_start(out=words[0][:].bitcast(I32), in_=tail_words[0].bitcast(I32))
         nc.sync.dma_start(out=hid_raw[:], in_=hid.rearrange("(p t) q -> p t q", t=PACK))
         nc.sync.dma_start(out=head_raw[:], in_=head.rearrange("(p t) u -> p t u", t=PACK))
         nc.sync.dma_start(out=htail_raw[:], in_=htail.rearrange("(z p t) q -> p z t q", p=P, t=PACK))
-        nc.sync.dma_start(out=first_words[:].bitcast(I32), in_=tail_words[0].bitcast(I32))
+        nc.sync.dma_start(out=words[1][:].bitcast(I32), in_=tail_words[1].bitcast(I32))
         nc.sync.dma_start(cluster_list[:], offs2)
 
         picked_scales = sb.tile([P, I], U8, name="picked_scales", align_bytes=64)
         nc.vector.tensor_copy(picked_scales[:], scale_rows[:].indirect(word_list[:]))
+        for quad in range(4):
+            first = 96 + 8 * quad
+            nc.sync.dma_start(
+                out=tail_planes[32 * quad : 32 * quad + 4, :].bitcast(I32),
+                in_=picked_scales[first : first + 8, :].bitcast(I32),
+            )
+        tl_sb = sb.tile([P, U], F32, name="tl_sb", tag="rows_then_tl", align_bytes=64)
+        nc.sync.dma_start(out=tl_sb[:], in_=tl)
 
-        def place_scale_rows(z):
-            for quad in range(4):
-                first = 96 + 16 * z + 4 * quad
-                nc.sync.dma_start(
-                    out=tail_planes[z][32 * quad : 32 * quad + 4, :].bitcast(I32),
-                    in_=picked_scales[first : first + 4, :].bitcast(I32),
-                )
-
-        place_scale_rows(0)
-        second_words = sb.tile([P, T], U16, name="second_words", tag="rows_then_words", align_bytes=64)
-        nc.sync.dma_start(out=second_words[:].bitcast(I32), in_=tail_words[1].bitcast(I32))
-        place_scale_rows(1)
+        first_pass = sb.tile([P, I], U16, name="first_pass", align_bytes=64)
+        nc.vector.tensor_copy(first_pass[:], words[0][:].indirect(word_list[:]))
 
         head_g = [sb.tile([P, half, PACK], BF16, name=f"head_g{h}", align_bytes=64) for h in range(2)]
         hid_g = sb.tile([P, Q, PACK], BF16, name="hid_g", align_bytes=64)
-        head_codes = sb.tile([P, U], U32, name="head_codes", tag="codes_then_words", align_bytes=64)
+        head_codes = sb.tile([P, U], U32, name="head_codes", align_bytes=64)
         head_plane = sb.tile([P, U], U8, name="head_plane", align_bytes=64)
         hid_codes = sb.tile([P, Q], U32, name="hid_codes", align_bytes=64)
         hid_plane = sb.tile([P, Q], U8, name="hid_plane", align_bytes=64)
         interleave(nc.scalar.copy, hid_g[:], hid_raw[:])
         interleave(nc.vector.tensor_copy, head_g[0][:], head_raw[:, :, 0:half])
         interleave(nc.scalar.copy, head_g[1][:], head_raw[:, :, half:U])
-        tl_sb = sb.tile([P, U], F32, name="tl_sb", tag="head_then_tl")
-        nc.sync.dma_start(out=tl_sb[:], in_=tl)
         quantise(nc, hid_codes[:], hid_plane[:], hid_g[:])
         a = ps.tile([P, U], F32, name="a")
         for h in range(2):
@@ -105,8 +102,14 @@ def tile_attend_adaptivesoftmax_kernel(tc, hid, head, tl, htail, tail_words, tai
                 out=a[:, us], lhsT=hid_codes[:].bitcast(FP8X4), lhsT_scale=hid_plane[:],
                 rhs=head_codes[:, us].bitcast(FP8X4), rhs_scale=head_plane[:, us], start=True, stop=True,
             )
+        htail_g = sb.tile([P, PASSES * Q, PACK], BF16, name="htail_g", align_bytes=64)
+        htail_codes = sb.tile([P, PASSES * Q], U32, name="htail_codes", align_bytes=64)
+        htail_plane = sb.tile([P, PASSES * Q], U8, name="htail_plane", align_bytes=64)
+        for z in range(PASSES):
+            interleave(nc.scalar.copy, htail_g[:, z * Q : (z + 1) * Q, :], htail_raw[:, z, :, :])
         neg_max = sb.tile([P, 1], F32, name="neg_max")
         nc.vector.tensor_reduce(out=neg_max[:], in_=a[:], axis=mybir.AxisListType.X, op=ALU.max, negate=True)
+        quantise(nc, htail_codes[:], htail_plane[:], htail_g[:])
         exps = sb.tile([P, U], F32, name="exps")
         row_sum = sb.tile([P, 1], F32, name="row_sum")
         nc.scalar.activation(out=exps[:], in_=a[:], func=ACT.Exp, bias=neg_max[:], accum_out=row_sum[:])
@@ -115,48 +118,39 @@ def tile_attend_adaptivesoftmax_kernel(tc, hid, head, tl, htail, tail_words, tai
         neg_lse = sb.tile([P, 1], F32, name="neg_lse")
         nc.scalar.activation(out=neg_lse[:], in_=log_sum[:], func=ACT.Identity, scale=-1.0, bias=neg_max[:])
 
-        htail_g = sb.tile([P, PASSES * Q, PACK], BF16, name="htail_g", align_bytes=64)
-        htail_codes = sb.tile([P, PASSES * Q], U32, name="htail_codes", align_bytes=64)
-        htail_plane = sb.tile([P, PASSES * Q], U8, name="htail_plane", align_bytes=64)
-        for z in range(PASSES):
-            qs = slice(z * Q, (z + 1) * Q)
-            interleave(nc.scalar.copy, htail_g[:, qs, :], htail_raw[:, z, :, :])
-            quantise(nc, htail_codes[:, qs], htail_plane[:, qs], htail_g[:, qs, :])
 
-        first_pass = sb.tile([P, I], U16, name="first_pass", tag="codes_then_words", align_bytes=64)
-        nc.vector.tensor_copy(first_pass[:], first_words[:].indirect(word_list[:]))
-        second_pass = [
-            sb.tile([P, BANK], U16, name="second_pass0", align_bytes=64),
-            sb.tile([P, BANK], U16, name="second_pass1", align_bytes=64),
-        ]
+        second_pass = []
         for h in range(I // BANK):
-            nc.vector.tensor_copy(
-                second_pass[h][:], second_words[:].indirect(word_list[:, h * BANK // 16 : (h + 1) * BANK // 16])
-            )
+            picked = sb.tile([P, BANK], U16, name=f"second_pass{h}", align_bytes=64)
+            second_pass.append(picked)
+            nc.vector.tensor_copy(picked[:], words[1][:].indirect(word_list[:, h * BANK // 16 : (h + 1) * BANK // 16]))
 
         nc.vector.scalar_tensor_tensor(
             out=b[:, 0:U], in0=a[:], scalar=neg_lse[:], in1=tl_sb[:], op0=ALU.add, op1=ALU.subtract
         )
 
         r = sb.tile([P, I], F32, name="r")
-        for h in range(I // BANK):
-            cols = slice(h * BANK, (h + 1) * BANK)
-            r_bank = ps.tile([P, BANK], F32, name=f"r_bank{h}")
-            for z in range(PASSES):
+        r_bank = [ps.tile([P, BANK], F32, name=f"r_bank{h}") for h in range(I // BANK)]
+        for z in range(PASSES):
+            for h in range(I // BANK):
+                cols = slice(h * BANK, (h + 1) * BANK)
                 nc.tensor.matmul_mx(
-                    out=r_bank[:],
+                    out=r_bank[h][:],
                     lhsT=htail_codes[:, z * Q : (z + 1) * Q].bitcast(FP8X4),
                     lhsT_scale=htail_plane[:, z * Q : (z + 1) * Q],
                     rhs=(first_pass[:, cols], second_pass[h][:])[z].bitcast(FP4X4),
-                    rhs_scale=tail_planes[z][:, cols],
+                    rhs_scale=tail_planes[:, z * I + h * BANK : z * I + (h + 1) * BANK],
                     start=(z == 0),
                     stop=(z == PASSES - 1),
                 )
-            nc.scalar.copy(out=r[:, cols], in_=r_bank[:])
+        for first, last in ((0, 512), (512, 1024)):
+            h = first // BANK
+            nc.scalar.copy(out=r[:, first:last], in_=r_bank[h][:, first - h * BANK : last - h * BANK])
 
+        result = sb.tile([P, I], F32, name="result")
         for first, last in PIECES:
-            result = sb.tile([P, last - first], F32, name=f"result{first}")
             nc.vector.tensor_tensor(
-                result[:], b[:].indirect(cluster_list[:, first // 16 : last // 16]), r[:, first:last], ALU.add
+                result[:, first:last], b[:].indirect(cluster_list[:, first // 16 : last // 16]), r[:, first:last], ALU.add
             )
-            nc.sync.dma_start(out=out[:, first:last], in_=result[:])
+        for first, last in STORES:
+            nc.sync.dma_start(out=out[:, first:last], in_=result[:, first:last])

@@ -21,8 +21,7 @@ PACK = 4
 PASSES = K // (P * PACK)
 BANK = 512
 LIST_COLS = I // 16
-SPARE = 32
-PIECES = ((0, 512), (512, 896), (896, 1024))
+PIECES = ((0, 128), (128, 512), (512, 768), (768, 896), (896, 1024))
 STORES = ((0, 512), (512, 896), (896, 1024))
 
 
@@ -47,11 +46,11 @@ def tile_attend_adaptivesoftmax_kernel(tc, hid, head, tl, htail, tail_words, tai
         cluster_list = sb.tile([P, LIST_COLS], U16, name="cluster_list")
         scale_rows = sb.tile([P, T], U8, name="scale_rows", tag="rows_then_tl", align_bytes=64)
         words = [sb.tile([P, T], U16, name=f"words{z}", align_bytes=64) for z in range(PASSES)]
-        htail_raw = sb.tile([P, PASSES, PACK, Q], F32, name="htail_raw")
+        htail_raw = [sb.tile([P, PACK, Q], F32, name=f"htail_raw{z}") for z in range(PASSES)]
         half = U // 2
         head_raw = sb.tile([P, PACK, U], F32, name="head_raw")
         hid_raw = sb.tile([P, PACK, Q], F32, name="hid_raw")
-        b = sb.tile([P, U + SPARE], F32, name="b")
+        b = sb.tile([P, U], F32, name="b")
         tail_planes = sb.tile([P, PASSES * I], U8, name="tail_planes", align_bytes=64)
 
         nc.vector.memset(scale_rows[0:96, :].bitcast(I32), 0)
@@ -60,14 +59,15 @@ def tile_attend_adaptivesoftmax_kernel(tc, hid, head, tl, htail, tail_words, tai
             in_=tail_scales.bitcast(I32).rearrange("z f t -> f z t"),
         )
         nc.vector.memset(tail_planes[:].bitcast(I32), 0)
-        nc.vector.memset(b[:, U:], 0.0)
 
         nc.sync.dma_start(word_list[:], offs)
-        nc.sync.dma_start(out=words[0][:].bitcast(I32), in_=tail_words[0].bitcast(I32))
         nc.sync.dma_start(out=hid_raw[:], in_=hid.rearrange("(p t) q -> p t q", t=PACK))
         nc.sync.dma_start(out=head_raw[:], in_=head.rearrange("(p t) u -> p t u", t=PACK))
-        nc.sync.dma_start(out=htail_raw[:], in_=htail.rearrange("(z p t) q -> p z t q", p=P, t=PACK))
-        nc.sync.dma_start(out=words[1][:].bitcast(I32), in_=tail_words[1].bitcast(I32))
+        htail_rows = htail.rearrange("(z p t) q -> z p t q", p=P, t=PACK)
+        for z in range(PASSES):
+            nc.sync.dma_start(out=htail_raw[z][:], in_=htail_rows[z])
+        for z in range(PASSES):
+            nc.sync.dma_start(out=words[z][:].bitcast(I32), in_=tail_words[z].bitcast(I32))
         nc.sync.dma_start(cluster_list[:], offs2)
 
         picked_scales = sb.tile([P, I], U8, name="picked_scales", align_bytes=64)
@@ -81,12 +81,9 @@ def tile_attend_adaptivesoftmax_kernel(tc, hid, head, tl, htail, tail_words, tai
         tl_sb = sb.tile([P, U], F32, name="tl_sb", tag="rows_then_tl", align_bytes=64)
         nc.sync.dma_start(out=tl_sb[:], in_=tl)
 
-        first_pass = sb.tile([P, I], U16, name="first_pass", align_bytes=64)
-        nc.vector.tensor_copy(first_pass[:], words[0][:].indirect(word_list[:]))
-
         head_g = [sb.tile([P, half, PACK], BF16, name=f"head_g{h}", align_bytes=64) for h in range(2)]
         hid_g = sb.tile([P, Q, PACK], BF16, name="hid_g", align_bytes=64)
-        head_codes = sb.tile([P, U], U32, name="head_codes", align_bytes=64)
+        head_codes = sb.tile([P, U], U32, name="head_codes", tag="codes_then_words", align_bytes=64)
         head_plane = sb.tile([P, U], U8, name="head_plane", align_bytes=64)
         hid_codes = sb.tile([P, Q], U32, name="hid_codes", align_bytes=64)
         hid_plane = sb.tile([P, Q], U8, name="hid_plane", align_bytes=64)
@@ -94,56 +91,73 @@ def tile_attend_adaptivesoftmax_kernel(tc, hid, head, tl, htail, tail_words, tai
         interleave(nc.vector.tensor_copy, head_g[0][:], head_raw[:, :, 0:half])
         interleave(nc.scalar.copy, head_g[1][:], head_raw[:, :, half:U])
         quantise(nc, hid_codes[:], hid_plane[:], hid_g[:])
-        a = ps.tile([P, U], F32, name="a")
+        a = [ps.tile([P, half], F32, name=f"a{h}") for h in range(2)]
         for h in range(2):
             us = slice(h * half, (h + 1) * half)
             quantise(nc, head_codes[:, us], head_plane[:, us], head_g[h][:])
             nc.tensor.matmul_mx(
-                out=a[:, us], lhsT=hid_codes[:].bitcast(FP8X4), lhsT_scale=hid_plane[:],
+                out=a[h][:], lhsT=hid_codes[:].bitcast(FP8X4), lhsT_scale=hid_plane[:],
                 rhs=head_codes[:, us].bitcast(FP8X4), rhs_scale=head_plane[:, us], start=True, stop=True,
             )
-        htail_g = sb.tile([P, PASSES * Q, PACK], BF16, name="htail_g", align_bytes=64)
-        htail_codes = sb.tile([P, PASSES * Q], U32, name="htail_codes", align_bytes=64)
-        htail_plane = sb.tile([P, PASSES * Q], U8, name="htail_plane", align_bytes=64)
+        htail_codes = [sb.tile([P, Q], U32, name=f"htail_codes{z}", align_bytes=64) for z in range(PASSES)]
+        htail_plane = [sb.tile([P, Q], U8, name=f"htail_plane{z}", align_bytes=64) for z in range(PASSES)]
+        htail_g = [
+            sb.tile([P, Q, PACK], BF16, name=f"htail_g{z}", align_bytes=64) for z in range(PASSES)
+        ]
         for z in range(PASSES):
-            interleave(nc.scalar.copy, htail_g[:, z * Q : (z + 1) * Q, :], htail_raw[:, z, :, :])
+            interleave(nc.scalar.copy, htail_g[z][:], htail_raw[z][:])
+        quantise(nc, htail_codes[0][:], htail_plane[0][:], htail_g[0][:])
+
+        neg_half_max = sb.tile([P, 1], F32, name="neg_half_max")
         neg_max = sb.tile([P, 1], F32, name="neg_max")
-        nc.vector.tensor_reduce(out=neg_max[:], in_=a[:], axis=mybir.AxisListType.X, op=ALU.max, negate=True)
-        quantise(nc, htail_codes[:], htail_plane[:], htail_g[:])
+        neg_a1 = sb.tile([P, half], F32, name="neg_a1")
+        nc.vector.tensor_reduce(out=neg_half_max[:], in_=a[0][:], axis=mybir.AxisListType.X, op=ALU.max, negate=True)
+        nc.vector.tensor_scalar(
+            out=neg_a1[:], in0=a[1][:], scalar1=-1.0, scalar2=neg_half_max[:], op0=ALU.mult, op1=ALU.min, accum_out=neg_max[:]
+        )
+        quantise(nc, htail_codes[1][:], htail_plane[1][:], htail_g[1][:])
         exps = sb.tile([P, U], F32, name="exps")
-        row_sum = sb.tile([P, 1], F32, name="row_sum")
-        nc.scalar.activation(out=exps[:], in_=a[:], func=ACT.Exp, bias=neg_max[:], accum_out=row_sum[:])
+        half_sum = [sb.tile([P, 1], F32, name=f"half_sum{h}") for h in range(2)]
+        rescale = sb.tile([P, 1], F32, name="rescale")
+        nc.scalar.activation(out=exps[:, 0:half], in_=a[0][:], func=ACT.Exp, bias=neg_half_max[:], accum_out=half_sum[0][:])
+        nc.scalar.activation(out=rescale[:], in_=neg_half_max[:], func=ACT.Exp, scale=-1.0, bias=neg_max[:])
+        nc.scalar.activation(
+            out=exps[:, half:U], in_=neg_a1[:], func=ACT.Exp, scale=-1.0, bias=neg_max[:], accum_out=half_sum[1][:]
+        )
         log_sum = sb.tile([P, 1], F32, name="log_sum")
-        nc.scalar.activation(out=log_sum[:], in_=row_sum[:], func=ACT.Ln)
+        nc.scalar.activation(out=log_sum[:], in_=half_sum[0][:], func=ACT.Ln, scale=rescale[:], bias=half_sum[1][:])
         neg_lse = sb.tile([P, 1], F32, name="neg_lse")
         nc.scalar.activation(out=neg_lse[:], in_=log_sum[:], func=ACT.Identity, scale=-1.0, bias=neg_max[:])
 
+        first_pass = sb.tile([P, I], U16, name="first_pass", tag="codes_then_words", align_bytes=64)
+        nc.vector.tensor_copy(first_pass[:], words[0][:].indirect(word_list[:]))
+        early = sb.tile([P, BANK], U16, name="second_pass0", align_bytes=64)
+        nc.vector.tensor_copy(early[:], words[1][:].indirect(word_list[:, 0 : BANK // 16]))
+        late = sb.tile([P, BANK], U16, name="second_pass1", align_bytes=64)
+        nc.vector.tensor_copy(late[:], words[1][:].indirect(word_list[:, BANK // 16 : I // 16]))
+        second_pass = [early, late]
 
-        second_pass = []
-        for h in range(I // BANK):
-            picked = sb.tile([P, BANK], U16, name=f"second_pass{h}", align_bytes=64)
-            second_pass.append(picked)
-            nc.vector.tensor_copy(picked[:], words[1][:].indirect(word_list[:, h * BANK // 16 : (h + 1) * BANK // 16]))
-
-        nc.vector.scalar_tensor_tensor(
-            out=b[:, 0:U], in0=a[:], scalar=neg_lse[:], in1=tl_sb[:], op0=ALU.add, op1=ALU.subtract
-        )
+        log_prob = sb.tile([P, U], F32, name="log_prob")
+        for h in range(2):
+            us = slice(h * half, (h + 1) * half)
+            nc.scalar.activation(out=log_prob[:, us], in_=a[h][:], func=ACT.Identity, bias=neg_lse[:])
+        nc.gpsimd.tensor_tensor(out=b[:], in0=log_prob[:], in1=tl_sb[:], op=ALU.subtract)
 
         r = sb.tile([P, I], F32, name="r")
         r_bank = [ps.tile([P, BANK], F32, name=f"r_bank{h}") for h in range(I // BANK)]
-        for z in range(PASSES):
-            for h in range(I // BANK):
+        for h in range(I // BANK):
+            for z in range(PASSES):
                 cols = slice(h * BANK, (h + 1) * BANK)
                 nc.tensor.matmul_mx(
                     out=r_bank[h][:],
-                    lhsT=htail_codes[:, z * Q : (z + 1) * Q].bitcast(FP8X4),
-                    lhsT_scale=htail_plane[:, z * Q : (z + 1) * Q],
+                    lhsT=htail_codes[z][:].bitcast(FP8X4),
+                    lhsT_scale=htail_plane[z][:],
                     rhs=(first_pass[:, cols], second_pass[h][:])[z].bitcast(FP4X4),
                     rhs_scale=tail_planes[:, z * I + h * BANK : z * I + (h + 1) * BANK],
                     start=(z == 0),
                     stop=(z == PASSES - 1),
                 )
-        for first, last in ((0, 512), (512, 1024)):
+        for first, last in ((0, 128), (128, 512), (512, 768), (768, 1024)):
             h = first // BANK
             nc.scalar.copy(out=r[:, first:last], in_=r_bank[h][:, first - h * BANK : last - h * BANK])
 

@@ -64,10 +64,10 @@ def tile_attend_adaptivesoftmax_kernel(tc, hid, head, tl, htail, tail_words, tai
         nc.sync.dma_start(out=hid_raw[:], in_=hid.rearrange("(p t) q -> p t q", t=PACK))
         nc.sync.dma_start(out=head_raw[:], in_=head.rearrange("(p t) u -> p t u", t=PACK))
         htail_rows = htail.rearrange("(z p t) q -> z p t q", p=P, t=PACK)
-        for z in range(PASSES):
-            nc.sync.dma_start(out=htail_raw[z][:], in_=htail_rows[z])
+        nc.sync.dma_start(out=htail_raw[0][:], in_=htail_rows[0])
         for z in range(PASSES):
             nc.sync.dma_start(out=words[z][:].bitcast(I32), in_=tail_words[z].bitcast(I32))
+        nc.sync.dma_start(out=htail_raw[1][:], in_=htail_rows[1])
         nc.sync.dma_start(cluster_list[:], offs2)
 
         picked_scales = sb.tile([P, I], U8, name="picked_scales", align_bytes=64)
@@ -102,10 +102,12 @@ def tile_attend_adaptivesoftmax_kernel(tc, hid, head, tl, htail, tail_words, tai
         htail_codes = [sb.tile([P, Q], U32, name=f"htail_codes{z}", align_bytes=64) for z in range(PASSES)]
         htail_plane = [sb.tile([P, Q], U8, name=f"htail_plane{z}", align_bytes=64) for z in range(PASSES)]
         htail_g = [
-            sb.tile([P, Q, PACK], BF16, name=f"htail_g{z}", align_bytes=64) for z in range(PASSES)
+            sb.tile([P, Q, PACK], BF16, name=f"htail_g{z}", tag=f"grouped{z}", align_bytes=64) for z in range(PASSES)
         ]
-        for z in range(PASSES):
-            interleave(nc.scalar.copy, htail_g[z][:], htail_raw[z][:])
+        interleave(nc.scalar.copy, htail_g[0][:], htail_raw[0][:])
+        nc.gpsimd.tensor_scalar(
+            out=htail_g[1][:], in0=htail_raw[1][:].rearrange("p t c -> p c t"), scalar1=1.0, scalar2=0.0, op0=ALU.mult, op1=ALU.add
+        )
         quantise(nc, htail_codes[0][:], htail_plane[0][:], htail_g[0][:])
 
         neg_half_max = sb.tile([P, 1], F32, name="neg_half_max")
@@ -115,7 +117,6 @@ def tile_attend_adaptivesoftmax_kernel(tc, hid, head, tl, htail, tail_words, tai
         nc.vector.tensor_scalar(
             out=neg_a1[:], in0=a[1][:], scalar1=-1.0, scalar2=neg_half_max[:], op0=ALU.mult, op1=ALU.min, accum_out=neg_max[:]
         )
-        quantise(nc, htail_codes[1][:], htail_plane[1][:], htail_g[1][:])
         exps = sb.tile([P, U], F32, name="exps")
         half_sum = [sb.tile([P, 1], F32, name=f"half_sum{h}") for h in range(2)]
         rescale = sb.tile([P, 1], F32, name="rescale")
@@ -133,7 +134,8 @@ def tile_attend_adaptivesoftmax_kernel(tc, hid, head, tl, htail, tail_words, tai
         nc.vector.tensor_copy(first_pass[:], words[0][:].indirect(word_list[:]))
         early = sb.tile([P, BANK], U16, name="second_pass0", align_bytes=64)
         nc.vector.tensor_copy(early[:], words[1][:].indirect(word_list[:, 0 : BANK // 16]))
-        late = sb.tile([P, BANK], U16, name="second_pass1", align_bytes=64)
+        quantise(nc, htail_codes[1][:], htail_plane[1][:], htail_g[1][:])
+        late = sb.tile([P, BANK], U16, name="second_pass1", tag="grouped1", align_bytes=64)
         nc.vector.tensor_copy(late[:], words[1][:].indirect(word_list[:, BANK // 16 : I // 16]))
         second_pass = [early, late]
 
@@ -141,7 +143,7 @@ def tile_attend_adaptivesoftmax_kernel(tc, hid, head, tl, htail, tail_words, tai
         for h in range(2):
             us = slice(h * half, (h + 1) * half)
             nc.scalar.activation(out=log_prob[:, us], in_=a[h][:], func=ACT.Identity, bias=neg_lse[:])
-        nc.gpsimd.tensor_tensor(out=b[:], in0=log_prob[:], in1=tl_sb[:], op=ALU.subtract)
+            nc.gpsimd.tensor_tensor(out=b[:, us], in0=log_prob[:, us], in1=tl_sb[:, us], op=ALU.subtract)
 
         r = sb.tile([P, I], F32, name="r")
         r_bank = [ps.tile([P, BANK], F32, name=f"r_bank{h}") for h in range(I // BANK)]

@@ -21,8 +21,8 @@ PACK = 4
 PASSES = K // (P * PACK)
 BANK = 512
 LIST_COLS = I // 16
-PIECES = ((0, 128), (128, 512), (512, 768), (768, 896), (896, 1024))
-STORES = ((0, 512), (512, 896), (896, 1024))
+PIECES = ((0, 128), (128, 512), (512, 768), (768, 960), (960, 1024))
+STORES = ((0, 512), (512, 768), (768, 960), (960, 1024))
 
 
 def interleave(copy, grouped, raw):
@@ -64,10 +64,9 @@ def tile_attend_adaptivesoftmax_kernel(tc, hid, head, tl, htail, tail_words, tai
         nc.sync.dma_start(out=hid_raw[:], in_=hid.rearrange("(p t) q -> p t q", t=PACK))
         nc.sync.dma_start(out=head_raw[:], in_=head.rearrange("(p t) u -> p t u", t=PACK))
         htail_rows = htail.rearrange("(z p t) q -> z p t q", p=P, t=PACK)
-        nc.sync.dma_start(out=htail_raw[0][:], in_=htail_rows[0])
         for z in range(PASSES):
+            nc.sync.dma_start(out=htail_raw[z][:], in_=htail_rows[z])
             nc.sync.dma_start(out=words[z][:].bitcast(I32), in_=tail_words[z].bitcast(I32))
-        nc.sync.dma_start(out=htail_raw[1][:], in_=htail_rows[1])
         nc.sync.dma_start(cluster_list[:], offs2)
 
         picked_scales = sb.tile([P, I], U8, name="picked_scales", align_bytes=64)
@@ -102,7 +101,7 @@ def tile_attend_adaptivesoftmax_kernel(tc, hid, head, tl, htail, tail_words, tai
         htail_codes = [sb.tile([P, Q], U32, name=f"htail_codes{z}", align_bytes=64) for z in range(PASSES)]
         htail_plane = [sb.tile([P, Q], U8, name=f"htail_plane{z}", align_bytes=64) for z in range(PASSES)]
         htail_g = [
-            sb.tile([P, Q, PACK], BF16, name=f"htail_g{z}", tag=f"grouped{z}", align_bytes=64) for z in range(PASSES)
+            sb.tile([P, Q, PACK], BF16, name=f"htail_g{z}", align_bytes=64) for z in range(PASSES)
         ]
         interleave(nc.scalar.copy, htail_g[0][:], htail_raw[0][:])
         nc.gpsimd.tensor_scalar(
@@ -132,10 +131,10 @@ def tile_attend_adaptivesoftmax_kernel(tc, hid, head, tl, htail, tail_words, tai
 
         first_pass = sb.tile([P, I], U16, name="first_pass", tag="codes_then_words", align_bytes=64)
         nc.vector.tensor_copy(first_pass[:], words[0][:].indirect(word_list[:]))
+        quantise(nc, htail_codes[1][:], htail_plane[1][:], htail_g[1][:])
         early = sb.tile([P, BANK], U16, name="second_pass0", align_bytes=64)
         nc.vector.tensor_copy(early[:], words[1][:].indirect(word_list[:, 0 : BANK // 16]))
-        quantise(nc, htail_codes[1][:], htail_plane[1][:], htail_g[1][:])
-        late = sb.tile([P, BANK], U16, name="second_pass1", tag="grouped1", align_bytes=64)
+        late = sb.tile([P, BANK], U16, name="second_pass1", align_bytes=64)
         nc.vector.tensor_copy(late[:], words[1][:].indirect(word_list[:, BANK // 16 : I // 16]))
         second_pass = [early, late]
 

@@ -20,6 +20,7 @@ P = 128
 PACK = 4
 PASSES = K // (P * PACK)
 BANK = 512
+GROUP = 128
 LIST_COLS = I // 16
 PIECES = ((0, 128), (128, 512), (512, 768), (768, 960), (960, 1024))
 STORES = ((0, 512), (512, 768), (768, 960), (960, 1024))
@@ -90,7 +91,7 @@ def tile_attend_adaptivesoftmax_kernel(tc, hid, head, tl, htail, tail_words, tai
         interleave(nc.vector.tensor_copy, head_g[0][:], head_raw[:, :, 0:half])
         interleave(nc.scalar.copy, head_g[1][:], head_raw[:, :, half:U])
         quantise(nc, hid_codes[:], hid_plane[:], hid_g[:])
-        a = [ps.tile([P, half], F32, name=f"a{h}") for h in range(2)]
+        a = [ps.tile([P, half], F32, name=f"a{h}", tag=f"bank{6 + h}") for h in range(2)]
         for h in range(2):
             us = slice(h * half, (h + 1) * half)
             quantise(nc, head_codes[:, us], head_plane[:, us], head_g[h][:])
@@ -142,25 +143,26 @@ def tile_attend_adaptivesoftmax_kernel(tc, hid, head, tl, htail, tail_words, tai
         for h in range(2):
             us = slice(h * half, (h + 1) * half)
             nc.scalar.activation(out=log_prob[:, us], in_=a[h][:], func=ACT.Identity, bias=neg_lse[:])
-            nc.gpsimd.tensor_tensor(out=b[:, us], in0=log_prob[:, us], in1=tl_sb[:, us], op=ALU.subtract)
+        nc.gpsimd.tensor_tensor(out=b[:], in0=log_prob[:], in1=tl_sb[:], op=ALU.subtract)
 
         r = sb.tile([P, I], F32, name="r")
-        r_bank = [ps.tile([P, BANK], F32, name=f"r_bank{h}") for h in range(I // BANK)]
+        per_half = BANK // GROUP
+        r_bank = [ps.tile([P, GROUP], F32, name=f"r_bank{g}", tag=f"bank{g}") for g in range(I // GROUP)]
         for h in range(I // BANK):
             for z in range(PASSES):
-                cols = slice(h * BANK, (h + 1) * BANK)
-                nc.tensor.matmul_mx(
-                    out=r_bank[h][:],
-                    lhsT=htail_codes[z][:].bitcast(FP8X4),
-                    lhsT_scale=htail_plane[z][:],
-                    rhs=(first_pass[:, cols], second_pass[h][:])[z].bitcast(FP4X4),
-                    rhs_scale=tail_planes[:, z * I + h * BANK : z * I + (h + 1) * BANK],
-                    start=(z == 0),
-                    stop=(z == PASSES - 1),
-                )
-        for first, last in ((0, 128), (128, 512), (512, 768), (768, 1024)):
-            h = first // BANK
-            nc.scalar.copy(out=r[:, first:last], in_=r_bank[h][:, first - h * BANK : last - h * BANK])
+                for j in range(per_half):
+                    first = h * BANK + j * GROUP
+                    nc.tensor.matmul_mx(
+                        out=r_bank[h * per_half + j][:],
+                        lhsT=htail_codes[z][:].bitcast(FP8X4),
+                        lhsT_scale=htail_plane[z][:],
+                        rhs=(first_pass[:, first : first + GROUP], second_pass[h][:, j * GROUP : (j + 1) * GROUP])[z].bitcast(FP4X4),
+                        rhs_scale=tail_planes[:, z * I + first : z * I + first + GROUP],
+                        start=(z == 0),
+                        stop=(z == PASSES - 1),
+                    )
+        for g in range(I // GROUP):
+            nc.scalar.copy(out=r[:, g * GROUP : (g + 1) * GROUP], in_=r_bank[g][:])
 
         result = sb.tile([P, I], F32, name="result")
         for first, last in PIECES:

@@ -47,7 +47,7 @@ def tile_attend_adaptivesoftmax_kernel(tc, hid, head, tl, htail, tail_words, tai
         cluster_list = sb.tile([P, LIST_COLS], U16, name="cluster_list")
         scale_rows = sb.tile([P, T], U8, name="scale_rows", tag="rows_then_tl", align_bytes=64)
         words = [sb.tile([P, T], U16, name=f"words{z}", align_bytes=64) for z in range(PASSES)]
-        htail_raw = [sb.tile([P, PACK, Q], F32, name=f"htail_raw{z}") for z in range(PASSES)]
+        htail_raw = sb.tile([P, PASSES, PACK, Q], F32, name="htail_raw")
         half = U // 2
         head_raw = sb.tile([P, PACK, U], F32, name="head_raw")
         hid_raw = sb.tile([P, PACK, Q], F32, name="hid_raw")
@@ -64,11 +64,12 @@ def tile_attend_adaptivesoftmax_kernel(tc, hid, head, tl, htail, tail_words, tai
         nc.sync.dma_start(word_list[:], offs)
         nc.sync.dma_start(out=hid_raw[:], in_=hid.rearrange("(p t) q -> p t q", t=PACK))
         nc.sync.dma_start(out=head_raw[:], in_=head.rearrange("(p t) u -> p t u", t=PACK))
-        htail_rows = htail.rearrange("(z p t) q -> z p t q", p=P, t=PACK)
-        for z in range(PASSES):
-            nc.sync.dma_start(out=htail_raw[z][:], in_=htail_rows[z])
-            nc.sync.dma_start(out=words[z][:].bitcast(I32), in_=tail_words[z].bitcast(I32))
+        nc.sync.dma_start(out=words[0][:].bitcast(I32), in_=tail_words[0].bitcast(I32))
+        nc.sync.dma_start(out=htail_raw[:], in_=htail.rearrange("(z p t) q -> p z t q", p=P, t=PACK))
+        nc.sync.dma_start(out=words[1][:].bitcast(I32), in_=tail_words[1].bitcast(I32))
         nc.sync.dma_start(cluster_list[:], offs2)
+        early_tl = sb.tile([P, half], F32, name="early_tl")
+        nc.sync.dma_start(out=early_tl[:], in_=tl[:, 0:half])
 
         picked_scales = sb.tile([P, I], U8, name="picked_scales", align_bytes=64)
         nc.vector.tensor_copy(picked_scales[:], scale_rows[:].indirect(word_list[:]))
@@ -78,8 +79,9 @@ def tile_attend_adaptivesoftmax_kernel(tc, hid, head, tl, htail, tail_words, tai
                 out=tail_planes[32 * quad : 32 * quad + 4, :].bitcast(I32),
                 in_=picked_scales[first : first + 8, :].bitcast(I32),
             )
-        tl_sb = sb.tile([P, U], F32, name="tl_sb", tag="rows_then_tl", align_bytes=64)
-        nc.sync.dma_start(out=tl_sb[:], in_=tl)
+        late_tl = sb.tile([P, half], F32, name="late_tl", tag="rows_then_tl", align_bytes=64)
+        nc.sync.dma_start(out=late_tl[:], in_=tl[:, half:U])
+        tl_sb = [early_tl, late_tl]
 
         head_g = [sb.tile([P, half, PACK], BF16, name=f"head_g{h}", align_bytes=64) for h in range(2)]
         hid_g = sb.tile([P, Q, PACK], BF16, name="hid_g", align_bytes=64)
@@ -99,16 +101,13 @@ def tile_attend_adaptivesoftmax_kernel(tc, hid, head, tl, htail, tail_words, tai
                 out=a[h][:], lhsT=hid_codes[:].bitcast(FP8X4), lhsT_scale=hid_plane[:],
                 rhs=head_codes[:, us].bitcast(FP8X4), rhs_scale=head_plane[:, us], start=True, stop=True,
             )
-        htail_codes = [sb.tile([P, Q], U32, name=f"htail_codes{z}", align_bytes=64) for z in range(PASSES)]
-        htail_plane = [sb.tile([P, Q], U8, name=f"htail_plane{z}", align_bytes=64) for z in range(PASSES)]
-        htail_g = [
-            sb.tile([P, Q, PACK], BF16, name=f"htail_g{z}", align_bytes=64) for z in range(PASSES)
-        ]
-        interleave(nc.scalar.copy, htail_g[0][:], htail_raw[0][:])
+        htail_codes = sb.tile([P, PASSES * Q], U32, name="htail_codes", align_bytes=64)
+        htail_plane = sb.tile([P, PASSES * Q], U8, name="htail_plane", align_bytes=64)
+        htail_g = sb.tile([P, PASSES * Q, PACK], BF16, name="htail_g", align_bytes=64)
         nc.gpsimd.tensor_scalar(
-            out=htail_g[1][:], in0=htail_raw[1][:].rearrange("p t c -> p c t"), scalar1=1.0, scalar2=0.0, op0=ALU.mult, op1=ALU.add
+            out=htail_g[:].rearrange("p (z c) t -> p z c t", z=PASSES), in0=htail_raw[:].rearrange("p z t c -> p z c t"),
+            scalar1=1.0, scalar2=0.0, op0=ALU.mult, op1=ALU.add,
         )
-        quantise(nc, htail_codes[0][:], htail_plane[0][:], htail_g[0][:])
 
         neg_half_max = sb.tile([P, 1], F32, name="neg_half_max")
         neg_max = sb.tile([P, 1], F32, name="neg_max")
@@ -132,7 +131,7 @@ def tile_attend_adaptivesoftmax_kernel(tc, hid, head, tl, htail, tail_words, tai
 
         first_pass = sb.tile([P, I], U16, name="first_pass", tag="codes_then_words", align_bytes=64)
         nc.vector.tensor_copy(first_pass[:], words[0][:].indirect(word_list[:]))
-        quantise(nc, htail_codes[1][:], htail_plane[1][:], htail_g[1][:])
+        quantise(nc, htail_codes[:], htail_plane[:], htail_g[:])
         early = sb.tile([P, BANK], U16, name="second_pass0", align_bytes=64)
         nc.vector.tensor_copy(early[:], words[1][:].indirect(word_list[:, 0 : BANK // 16]))
         late = sb.tile([P, BANK], U16, name="second_pass1", align_bytes=64)
@@ -143,7 +142,7 @@ def tile_attend_adaptivesoftmax_kernel(tc, hid, head, tl, htail, tail_words, tai
         for h in range(2):
             us = slice(h * half, (h + 1) * half)
             nc.scalar.activation(out=log_prob[:, us], in_=a[h][:], func=ACT.Identity, bias=neg_lse[:])
-        nc.gpsimd.tensor_tensor(out=b[:], in0=log_prob[:], in1=tl_sb[:], op=ALU.subtract)
+            nc.gpsimd.tensor_tensor(out=b[:, us], in0=log_prob[:, us], in1=tl_sb[h][:], op=ALU.subtract)
 
         r = sb.tile([P, I], F32, name="r")
         per_half = BANK // GROUP
@@ -154,8 +153,8 @@ def tile_attend_adaptivesoftmax_kernel(tc, hid, head, tl, htail, tail_words, tai
                     first = h * BANK + j * GROUP
                     nc.tensor.matmul_mx(
                         out=r_bank[h * per_half + j][:],
-                        lhsT=htail_codes[z][:].bitcast(FP8X4),
-                        lhsT_scale=htail_plane[z][:],
+                        lhsT=htail_codes[:, z * Q : (z + 1) * Q].bitcast(FP8X4),
+                        lhsT_scale=htail_plane[:, z * Q : (z + 1) * Q],
                         rhs=(first_pass[:, first : first + GROUP], second_pass[h][:, j * GROUP : (j + 1) * GROUP])[z].bitcast(FP4X4),
                         rhs_scale=tail_planes[:, z * I + first : z * I + first + GROUP],
                         start=(z == 0),

@@ -22,8 +22,10 @@ PASSES = K // (P * PACK)
 BANK = 512
 GROUP = 128
 LIST_COLS = I // 16
-PIECES = ((0, 128), (128, 512), (512, 768), (768, 960), (960, 1024))
-STORES = ((0, 512), (512, 768), (768, 960), (960, 1024))
+PIECES = ((0, 128), (128, 320), (320, 512))
+LOOK_UP = 256
+VECTOR_CASTS = 320
+STORES = ((0, 320), (320, 512), (512, 768), (768, 896), (896, 1024))
 
 
 def interleave(copy, grouped, raw):
@@ -91,7 +93,8 @@ def tile_attend_adaptivesoftmax_kernel(tc, hid, head, tl, htail, tail_words, tai
         hid_plane = sb.tile([P, Q], U8, name="hid_plane", align_bytes=64)
         interleave(nc.scalar.copy, hid_g[:], hid_raw[:])
         interleave(nc.vector.tensor_copy, head_g[0][:], head_raw[:, :, 0:half])
-        interleave(nc.scalar.copy, head_g[1][:], head_raw[:, :, half:U])
+        interleave(nc.vector.tensor_copy, head_g[1][:, 0 : VECTOR_CASTS - half, :], head_raw[:, :, half:VECTOR_CASTS])
+        interleave(nc.scalar.copy, head_g[1][:, VECTOR_CASTS - half : half, :], head_raw[:, :, VECTOR_CASTS:U])
         quantise(nc, hid_codes[:], hid_plane[:], hid_g[:])
         a = [ps.tile([P, half], F32, name=f"a{h}", tag=f"bank{6 + h}") for h in range(2)]
         for h in range(2):
@@ -144,7 +147,7 @@ def tile_attend_adaptivesoftmax_kernel(tc, hid, head, tl, htail, tail_words, tai
             nc.scalar.activation(out=log_prob[:, us], in_=a[h][:], func=ACT.Identity, bias=neg_lse[:])
             nc.gpsimd.tensor_tensor(out=b[:, us], in0=log_prob[:, us], in1=tl_sb[h][:], op=ALU.subtract)
 
-        r = sb.tile([P, I], F32, name="r")
+        r = sb.tile([P, BANK], F32, name="r")
         per_half = BANK // GROUP
         r_bank = [ps.tile([P, GROUP], F32, name=f"r_bank{g}", tag=f"bank{g}") for g in range(I // GROUP)]
         for h in range(I // BANK):
@@ -160,13 +163,25 @@ def tile_attend_adaptivesoftmax_kernel(tc, hid, head, tl, htail, tail_words, tai
                         start=(z == 0),
                         stop=(z == PASSES - 1),
                     )
-        for g in range(I // GROUP):
+        for g in range(per_half):
             nc.scalar.copy(out=r[:, g * GROUP : (g + 1) * GROUP], in_=r_bank[g][:])
+        picked_b = sb.tile([P, I - BANK], F32, name="picked_b")
+        for first in range(BANK, I, LOOK_UP):
+            nc.scalar.activation(
+                out=picked_b[:, first - BANK : first - BANK + LOOK_UP],
+                in_=b[:].indirect(cluster_list[:, first // 16 : (first + LOOK_UP) // 16]),
+                func=ACT.Copy,
+            )
 
         result = sb.tile([P, I], F32, name="result")
         for first, last in PIECES:
             nc.vector.tensor_tensor(
                 result[:, first:last], b[:].indirect(cluster_list[:, first // 16 : last // 16]), r[:, first:last], ALU.add
+            )
+        for g in range(per_half, I // GROUP):
+            first = g * GROUP
+            nc.vector.tensor_tensor(
+                result[:, first : first + GROUP], r_bank[g][:], picked_b[:, first - BANK : first - BANK + GROUP], ALU.add
             )
         for first, last in STORES:
             nc.sync.dma_start(out=out[:, first:last], in_=result[:, first:last])

@@ -75,14 +75,19 @@ def tile_attend_adaptivesoftmax_kernel(tc, hid, head, tl, htail, tail_words, tai
 
         picked_scales = sb.tile([P, I], U8, name="picked_scales", align_bytes=64)
         nc.vector.tensor_copy(picked_scales[:], scale_rows[:].indirect(word_list[:]))
-        for quad in range(4):
-            first = 96 + 8 * quad
-            nc.sync.dma_start(
-                out=tail_planes[32 * quad : 32 * quad + 4, :].bitcast(I32),
-                in_=picked_scales[first : first + 8, :].bitcast(I32),
-            )
+
+        def move_rows(h):
+            for quad in range(4):
+                first = 96 + 8 * quad
+                nc.sync.dma_start(
+                    out=tail_planes[32 * quad : 32 * quad + 4, h * PASSES * BANK : (h + 1) * PASSES * BANK].bitcast(I32),
+                    in_=picked_scales[first : first + 8, h * BANK : (h + 1) * BANK].bitcast(I32),
+                )
+
+        move_rows(0)
         late_tl = sb.tile([P, half], F32, name="late_tl", tag="rows_then_tl", align_bytes=64)
         nc.sync.dma_start(out=late_tl[:], in_=tl[:, half:U])
+        move_rows(1)
         tl_sb = [early_tl, late_tl]
 
         head_g = [sb.tile([P, half, PACK], BF16, name=f"head_g{h}", align_bytes=64) for h in range(2)]
@@ -152,6 +157,7 @@ def tile_attend_adaptivesoftmax_kernel(tc, hid, head, tl, htail, tail_words, tai
         r_bank = [ps.tile([P, GROUP], F32, name=f"r_bank{g}", tag=f"bank{g}") for g in range(I // GROUP)]
         for h in range(I // BANK):
             for z in range(PASSES):
+                plane = (h * PASSES + z) * BANK
                 for j in range(per_half):
                     first = h * BANK + j * GROUP
                     nc.tensor.matmul_mx(
@@ -159,7 +165,7 @@ def tile_attend_adaptivesoftmax_kernel(tc, hid, head, tl, htail, tail_words, tai
                         lhsT=htail_codes[:, z * Q : (z + 1) * Q].bitcast(FP8X4),
                         lhsT_scale=htail_plane[:, z * Q : (z + 1) * Q],
                         rhs=(first_pass[:, first : first + GROUP], second_pass[h][:, j * GROUP : (j + 1) * GROUP])[z].bitcast(FP4X4),
-                        rhs_scale=tail_planes[:, z * I + first : z * I + first + GROUP],
+                        rhs_scale=tail_planes[:, plane + j * GROUP : plane + (j + 1) * GROUP],
                         start=(z == 0),
                         stop=(z == PASSES - 1),
                     )

@@ -1,3 +1,4 @@
+import math
 from contextlib import ExitStack
 
 import concourse.mybir as mybir
@@ -19,13 +20,11 @@ ACT = mybir.ActivationFunctionType
 P = 128
 PACK = 4
 PASSES = K // (P * PACK)
-BANK = 512
-GROUP = 128
+HALF = I // 2
 LIST_COLS = I // 16
-PIECES = ((0, 128), (128, 320), (320, 512))
-LOOK_UP = 256
-VECTOR_CASTS = 320
-STORES = ((0, 320), (320, 512), (512, 768), (768, 896), (896, 1024))
+NODES = 96
+NODE_STEP = math.exp(-1.0)
+FIRST_NODE = -32.0
 
 
 def interleave(copy, grouped, raw):
@@ -39,6 +38,12 @@ def quantise(nc, codes, scales, grouped):
     nc.vector.quantize_mx(out=codes.bitcast(FP8X4), scales=scales, in_=grouped.rearrange("p c t -> p (c t)"))
 
 
+VECTOR_CASTS = 320
+LOOK_UP = 256
+GROUPS = ((0, 256), (256, 512), (512, 640), (640, 768), (768, 896), (896, 1024))
+STORES = ((256, 512), (0, 256), (512, 768), (768, 896), (896, 1024))
+
+
 def tile_attend_adaptivesoftmax_kernel(tc, hid, head, tl, htail, tail_words, tail_scales, offs, offs2, out):
     nc = tc.nc
     with ExitStack() as ctx:
@@ -47,12 +52,12 @@ def tile_attend_adaptivesoftmax_kernel(tc, hid, head, tl, htail, tail_words, tai
 
         word_list = sb.tile([P, LIST_COLS], U16, name="word_list")
         cluster_list = sb.tile([P, LIST_COLS], U16, name="cluster_list")
-        scale_rows = sb.tile([P, T], U8, name="scale_rows", tag="rows_then_tl", align_bytes=64)
+        scale_rows = sb.tile([P, T], U8, name="scale_rows", tag="raw_then_b1", align_bytes=64)
         words = [sb.tile([P, T], U16, name=f"words{z}", align_bytes=64) for z in range(PASSES)]
-        htail_raw = sb.tile([P, PASSES, PACK, Q], F32, name="htail_raw")
-        half = U // 2
+        htail_raw = [sb.tile([P, PACK, Q], F32, name=f"htail_raw{z}", tag=f"raw_then_b{z}", align_bytes=64) for z in range(1)]
         head_raw = sb.tile([P, PACK, U], F32, name="head_raw")
         hid_raw = sb.tile([P, PACK, Q], F32, name="hid_raw")
+        tl_sb = sb.tile([P, U], F32, name="tl_sb")
         b = sb.tile([P, U], F32, name="b")
         tail_planes = sb.tile([P, PASSES * I], U8, name="tail_planes", align_bytes=64)
 
@@ -66,42 +71,48 @@ def tile_attend_adaptivesoftmax_kernel(tc, hid, head, tl, htail, tail_words, tai
         nc.sync.dma_start(word_list[:], offs)
         nc.sync.dma_start(out=hid_raw[:], in_=hid.rearrange("(p t) q -> p t q", t=PACK))
         nc.sync.dma_start(out=head_raw[:], in_=head.rearrange("(p t) u -> p t u", t=PACK))
+        htail_rows = htail.rearrange("(z p t) q -> z p t q", p=P, t=PACK)
+        nc.sync.dma_start(out=htail_raw[0][:], in_=htail_rows[0])
+        nc.sync.dma_start(out=tl_sb[:], in_=tl)
         nc.sync.dma_start(out=words[0][:].bitcast(I32), in_=tail_words[0].bitcast(I32))
-        nc.sync.dma_start(out=htail_raw[:], in_=htail.rearrange("(z p t) q -> p z t q", p=P, t=PACK))
-        nc.sync.dma_start(out=words[1][:].bitcast(I32), in_=tail_words[1].bitcast(I32))
         nc.sync.dma_start(cluster_list[:], offs2)
-        early_tl = sb.tile([P, half], F32, name="early_tl")
-        nc.sync.dma_start(out=early_tl[:], in_=tl[:, 0:half])
+        nc.sync.dma_start(out=words[1][:].bitcast(I32), in_=tail_words[1].bitcast(I32))
+
+        steps = sb.tile([P, NODES], F32, name="steps")
+        nc.gpsimd.iota(steps[:], [[1, NODES]], base=0, channel_multiplier=0, allow_small_or_imprecise_dtypes=True)
+        nodes = sb.tile([P, NODES], F32, name="nodes")
+        nc.scalar.activation(out=nodes[:], in_=steps[:], func=ACT.Exp, scale=NODE_STEP, bias=FIRST_NODE)
+        neg_nodes = sb.tile([P, NODES], F32, name="neg_nodes")
+        nc.scalar.activation(out=neg_nodes[:], in_=nodes[:], func=ACT.Copy, scale=-1.0)
+        terms = sb.tile([P, NODES], F32, name="terms")
+        sum_at_one = sb.tile([P, 1], F32, name="sum_at_one")
+        nc.scalar.activation(out=terms[:], in_=neg_nodes[:], func=ACT.Exp, bias=-1.0, accum_out=sum_at_one[:])
 
         picked_scales = sb.tile([P, I], U8, name="picked_scales", align_bytes=64)
         nc.vector.tensor_copy(picked_scales[:], scale_rows[:].indirect(word_list[:]))
+        for quad in (0, 2, 1, 3):
+            first = 96 + 8 * quad
+            nc.sync.dma_start(
+                out=tail_planes[32 * quad : 32 * quad + 4, :].bitcast(I32),
+                in_=picked_scales[first : first + 8, :].bitcast(I32),
+            )
 
-        def move_rows(h):
-            for quad in range(4):
-                first = 96 + 8 * quad
-                nc.sync.dma_start(
-                    out=tail_planes[32 * quad : 32 * quad + 4, h * PASSES * BANK : (h + 1) * PASSES * BANK].bitcast(I32),
-                    in_=picked_scales[first : first + 8, h * BANK : (h + 1) * BANK].bitcast(I32),
-                )
+        htail_raw.append(sb.tile([P, PACK, Q], F32, name="htail_raw1", tag="raw_then_b1", align_bytes=64))
+        nc.sync.dma_start(out=htail_raw[1][:], in_=htail_rows[1])
 
-        move_rows(0)
-        late_tl = sb.tile([P, half], F32, name="late_tl", tag="rows_then_tl", align_bytes=64)
-        nc.sync.dma_start(out=late_tl[:], in_=tl[:, half:U])
-        move_rows(1)
-        tl_sb = [early_tl, late_tl]
-
+        half = U // 2
         head_g = [sb.tile([P, half, PACK], BF16, name=f"head_g{h}", align_bytes=64) for h in range(2)]
         hid_g = sb.tile([P, Q, PACK], BF16, name="hid_g", align_bytes=64)
         head_codes = sb.tile([P, U], U32, name="head_codes", tag="codes_then_words", align_bytes=64)
         head_plane = sb.tile([P, U], U8, name="head_plane", align_bytes=64)
-        hid_codes = sb.tile([P, Q], U32, name="hid_codes", align_bytes=64)
+        hid_codes = sb.tile([P, Q], U32, name="hid_codes", tag="hid_then_htail", align_bytes=64)
         hid_plane = sb.tile([P, Q], U8, name="hid_plane", align_bytes=64)
         interleave(nc.scalar.copy, hid_g[:], hid_raw[:])
         interleave(nc.vector.tensor_copy, head_g[0][:], head_raw[:, :, 0:half])
         interleave(nc.vector.tensor_copy, head_g[1][:, 0 : VECTOR_CASTS - half, :], head_raw[:, :, half:VECTOR_CASTS])
         interleave(nc.scalar.copy, head_g[1][:, VECTOR_CASTS - half : half, :], head_raw[:, :, VECTOR_CASTS:U])
         quantise(nc, hid_codes[:], hid_plane[:], hid_g[:])
-        a = [ps.tile([P, half], F32, name=f"a{h}", tag=f"bank{6 + h}") for h in range(2)]
+        a = [ps.tile([P, half], F32, name=f"a{h}") for h in range(2)]
         for h in range(2):
             us = slice(h * half, (h + 1) * half)
             quantise(nc, head_codes[:, us], head_plane[:, us], head_g[h][:])
@@ -109,85 +120,95 @@ def tile_attend_adaptivesoftmax_kernel(tc, hid, head, tl, htail, tail_words, tai
                 out=a[h][:], lhsT=hid_codes[:].bitcast(FP8X4), lhsT_scale=hid_plane[:],
                 rhs=head_codes[:, us].bitcast(FP8X4), rhs_scale=head_plane[:, us], start=True, stop=True,
             )
-        htail_codes = sb.tile([P, PASSES * Q], U32, name="htail_codes", align_bytes=64)
-        htail_plane = sb.tile([P, PASSES * Q], U8, name="htail_plane", align_bytes=64)
-        htail_g = sb.tile([P, PASSES * Q, PACK], BF16, name="htail_g", align_bytes=64)
-        nc.gpsimd.tensor_scalar(
-            out=htail_g[:].rearrange("p (z c) t -> p z c t", z=PASSES), in0=htail_raw[:].rearrange("p z t c -> p z c t"),
-            scalar1=1.0, scalar2=0.0, op0=ALU.mult, op1=ALU.add,
-        )
+        htail_codes = [None, sb.tile([P, Q], U32, name="htail_codes1", align_bytes=64)]
+        htail_plane = [sb.tile([P, Q], U8, name=f"htail_plane{z}", align_bytes=64) for z in range(PASSES)]
+        early_g = sb.tile([P, Q, PACK], BF16, name="early_g", align_bytes=64)
+        interleave(nc.scalar.copy, early_g[:], htail_raw[0][:])
 
+        neg_a = sb.tile([P, U], F32, name="neg_a")
         neg_half_max = sb.tile([P, 1], F32, name="neg_half_max")
         neg_max = sb.tile([P, 1], F32, name="neg_max")
-        neg_a1 = sb.tile([P, half], F32, name="neg_a1")
-        nc.vector.tensor_reduce(out=neg_half_max[:], in_=a[0][:], axis=mybir.AxisListType.X, op=ALU.max, negate=True)
         nc.vector.tensor_scalar(
-            out=neg_a1[:], in0=a[1][:], scalar1=-1.0, scalar2=neg_half_max[:], op0=ALU.mult, op1=ALU.min, accum_out=neg_max[:]
+            out=neg_a[:, 0:half], in0=a[0][:], scalar1=-1.0, scalar2=None, op0=ALU.mult, op1=ALU.min, accum_out=neg_half_max[:]
         )
+        nc.vector.tensor_scalar(
+            out=neg_a[:, half:U], in0=a[1][:], scalar1=-1.0, scalar2=neg_half_max[:], op0=ALU.mult, op1=ALU.min, accum_out=neg_max[:]
+        )
+        htail_codes[0] = sb.tile([P, Q], U32, name="htail_codes0", tag="hid_then_htail", align_bytes=64)
+        quantise(nc, htail_codes[0][:], htail_plane[0][:], early_g[:])
+        tl_less_a = sb.tile([P, U], F32, name="tl_less_a")
+        nc.gpsimd.tensor_tensor(out=tl_less_a[:], in0=neg_a[:], in1=tl_sb[:], op=ALU.add)
         exps = sb.tile([P, U], F32, name="exps")
-        half_sum = [sb.tile([P, 1], F32, name=f"half_sum{h}") for h in range(2)]
-        rescale = sb.tile([P, 1], F32, name="rescale")
-        nc.scalar.activation(out=exps[:, 0:half], in_=a[0][:], func=ACT.Exp, bias=neg_half_max[:], accum_out=half_sum[0][:])
-        nc.scalar.activation(out=rescale[:], in_=neg_half_max[:], func=ACT.Exp, scale=-1.0, bias=neg_max[:])
-        nc.scalar.activation(
-            out=exps[:, half:U], in_=neg_a1[:], func=ACT.Exp, scale=-1.0, bias=neg_max[:], accum_out=half_sum[1][:]
+        row_sum = sb.tile([P, 1], F32, name="row_sum")
+        nc.scalar.activation(out=exps[:], in_=neg_a[:], func=ACT.Exp, scale=-1.0, bias=neg_max[:], accum_out=row_sum[:])
+        base = sb.tile([P, 1], F32, name="base")
+        nc.scalar.activation(out=base[:], in_=sum_at_one[:], func=ACT.Identity, scale=-1.0, bias=neg_max[:])
+        row_terms = sb.tile([P, NODES], F32, name="row_terms")
+        sum_at_row = sb.tile([P, 1], F32, name="sum_at_row")
+        nc.scalar.activation(out=row_terms[:], in_=neg_nodes[:], func=ACT.Exp, scale=row_sum[:], bias=-1.0, accum_out=sum_at_row[:])
+        shift = sb.tile([P, 1], F32, name="shift")
+        nc.scalar.activation(out=shift[:], in_=sum_at_row[:], func=ACT.Identity, bias=base[:])
+        nc.gpsimd.tensor_scalar(
+            out=b[:, 0:half], in0=tl_less_a[:, 0:half], scalar1=-1.0, scalar2=shift[:], op0=ALU.mult, op1=ALU.add
         )
-        log_sum = sb.tile([P, 1], F32, name="log_sum")
-        nc.scalar.activation(out=log_sum[:], in_=half_sum[0][:], func=ACT.Ln, scale=rescale[:], bias=half_sum[1][:])
-        neg_lse = sb.tile([P, 1], F32, name="neg_lse")
-        nc.scalar.activation(out=neg_lse[:], in_=log_sum[:], func=ACT.Identity, scale=-1.0, bias=neg_max[:])
+        nc.scalar.activation(out=b[:, half:U], in_=tl_less_a[:, half:U], func=ACT.Identity, scale=-1.0, bias=shift[:])
 
         first_pass = sb.tile([P, I], U16, name="first_pass", tag="codes_then_words", align_bytes=64)
         nc.vector.tensor_copy(first_pass[:], words[0][:].indirect(word_list[:]))
-        quantise(nc, htail_codes[:], htail_plane[:], htail_g[:])
-        early = sb.tile([P, BANK], U16, name="second_pass0", align_bytes=64)
-        nc.vector.tensor_copy(early[:], words[1][:].indirect(word_list[:, 0 : BANK // 16]))
-        late = sb.tile([P, BANK], U16, name="second_pass1", align_bytes=64)
-        nc.vector.tensor_copy(late[:], words[1][:].indirect(word_list[:, BANK // 16 : I // 16]))
-        second_pass = [early, late]
+        early = sb.tile([P, HALF], U16, name="early", tag="words_then_b", align_bytes=64)
+        nc.vector.tensor_copy(early[:], words[1][:].indirect(word_list[:, 0 : HALF // 16]))
+        late_g = sb.tile([P, Q, PACK], BF16, name="late_g", tag="cast_then_words", align_bytes=64)
+        picked_b = {}
 
-        log_prob = sb.tile([P, U], F32, name="log_prob")
+        def look_up(first, last, tag):
+            tile = sb.tile([P, last - first], F32, name=f"picked_b{first}", tag=tag, align_bytes=64)
+            nc.scalar.activation(out=tile[:], in_=b[:].indirect(cluster_list[:, first // 16 : last // 16]), func=ACT.Copy)
+            for column in range(first, last, 128):
+                picked_b[column] = (tile, first)
+
+        def b_columns(first, last):
+            tile, start = picked_b[first]
+            return tile[:, first - start : last - start]
+
+        look_up(0, 256, "first_b")
+        look_up(640, 768, "second_b")
+        nc.gpsimd.tensor_scalar(
+            out=late_g[:, 0 : Q // 2, :], in0=htail_raw[1][:, :, 0 : Q // 2].rearrange("p t c -> p c t"),
+            scalar1=1.0, scalar2=0.0, op0=ALU.mult, op1=ALU.add,
+        )
+        interleave(nc.scalar.copy, late_g[:, Q // 2 : Q, :], htail_raw[1][:, :, Q // 2 : Q])
+        quantise(nc, htail_codes[1][:], htail_plane[1][:], late_g[:])
+        late = sb.tile([P, HALF], U16, name="late", tag="cast_then_words", align_bytes=64)
+        nc.vector.tensor_copy(late[:], words[1][:].indirect(word_list[:, HALF // 16 : I // 16]))
+        picked = [[first_pass[:, 0:HALF], first_pass[:, HALF:I]], [early[:], late[:]]]
+
+        look_up(256, 640, "raw_then_b1")
+
+        r_bank = [ps.tile([P, last - first], F32, name=f"r_bank{g}") for g, (first, last) in enumerate(GROUPS)]
         for h in range(2):
-            us = slice(h * half, (h + 1) * half)
-            nc.scalar.activation(out=log_prob[:, us], in_=a[h][:], func=ACT.Identity, bias=neg_lse[:])
-            nc.gpsimd.tensor_tensor(out=b[:, us], in0=log_prob[:, us], in1=tl_sb[h][:], op=ALU.subtract)
-
-        r = sb.tile([P, BANK], F32, name="r")
-        per_half = BANK // GROUP
-        r_bank = [ps.tile([P, GROUP], F32, name=f"r_bank{g}", tag=f"bank{g}") for g in range(I // GROUP)]
-        for h in range(I // BANK):
             for z in range(PASSES):
-                plane = (h * PASSES + z) * BANK
-                for j in range(per_half):
-                    first = h * BANK + j * GROUP
-                    nc.tensor.matmul_mx(
-                        out=r_bank[h * per_half + j][:],
-                        lhsT=htail_codes[:, z * Q : (z + 1) * Q].bitcast(FP8X4),
-                        lhsT_scale=htail_plane[:, z * Q : (z + 1) * Q],
-                        rhs=(first_pass[:, first : first + GROUP], second_pass[h][:, j * GROUP : (j + 1) * GROUP])[z].bitcast(FP4X4),
-                        rhs_scale=tail_planes[:, plane + j * GROUP : plane + (j + 1) * GROUP],
-                        start=(z == 0),
-                        stop=(z == PASSES - 1),
-                    )
-        for g in range(per_half):
-            nc.scalar.copy(out=r[:, g * GROUP : (g + 1) * GROUP], in_=r_bank[g][:])
-        picked_b = sb.tile([P, I - BANK], F32, name="picked_b")
-        for first in range(BANK, I, LOOK_UP):
-            nc.scalar.activation(
-                out=picked_b[:, first - BANK : first - BANK + LOOK_UP],
-                in_=b[:].indirect(cluster_list[:, first // 16 : (first + LOOK_UP) // 16]),
-                func=ACT.Copy,
-            )
+                for g, (first, last) in enumerate(GROUPS):
+                    if first // HALF == h:
+                        cols = slice(first - h * HALF, last - h * HALF)
+                        plane = z * I + h * HALF
+                        nc.tensor.matmul_mx(
+                            out=r_bank[g][:],
+                            lhsT=htail_codes[z][:].bitcast(FP8X4),
+                            lhsT_scale=htail_plane[z][:],
+                            rhs=picked[z][h][:, cols].bitcast(FP4X4),
+                            rhs_scale=tail_planes[:, plane + cols.start : plane + cols.stop],
+                            start=(z == 0),
+                            stop=(z == PASSES - 1),
+                        )
 
         result = sb.tile([P, I], F32, name="result")
-        for first, last in PIECES:
-            nc.vector.tensor_tensor(
-                result[:, first:last], b[:].indirect(cluster_list[:, first // 16 : last // 16]), r[:, first:last], ALU.add
-            )
-        for g in range(per_half, I // GROUP):
-            first = g * GROUP
-            nc.vector.tensor_tensor(
-                result[:, first : first + GROUP], r_bank[g][:], picked_b[:, first - BANK : first - BANK + GROUP], ALU.add
-            )
+        first, last = GROUPS[0]
+        r = sb.tile([P, last - first], F32, name="r")
+        nc.scalar.copy(out=r[:], in_=r_bank[0][:])
+        nc.gpsimd.tensor_tensor(out=result[:, first:last], in0=r[:], in1=b_columns(first, last), op=ALU.add)
+        look_up(768, 1024, "words_then_b")
+        for g in range(1, len(GROUPS)):
+            first, last = GROUPS[g]
+            nc.vector.tensor_tensor(result[:, first:last], r_bank[g][:], b_columns(first, last), ALU.add)
         for first, last in STORES:
             nc.sync.dma_start(out=out[:, first:last], in_=result[:, first:last])

@@ -48,12 +48,13 @@ def tile_attend_adaptivesoftmax_kernel(tc, hid, head, tl, htail, tail_words, tai
     nc = tc.nc
     with ExitStack() as ctx:
         sb = ctx.enter_context(tc.tile_pool(name="sb", bufs=1))
+        shared = ctx.enter_context(tc.tile_pool(name="shared", bufs=1))
         ps = ctx.enter_context(tc.psum_pool(name="ps", bufs=1))
 
         word_list = sb.tile([P, LIST_COLS], U16, name="word_list")
         cluster_list = sb.tile([P, LIST_COLS], U16, name="cluster_list")
-        scale_rows = sb.tile([P, T], U8, name="scale_rows", tag="raw_then_b1", align_bytes=64)
-        words = [sb.tile([P, T], U16, name=f"words{z}", align_bytes=64) for z in range(PASSES)]
+        scale_rows = shared.tile([P, T], U8, name="scale_rows", offset=6144, align_bytes=64)
+        words = [sb.tile([P, T], U16, name="words0", align_bytes=64)]
         htail_raw = [sb.tile([P, PACK, Q], F32, name=f"htail_raw{z}", tag=f"raw_then_b{z}", align_bytes=64) for z in range(1)]
         head_raw = sb.tile([P, PACK, U], F32, name="head_raw")
         hid_raw = sb.tile([P, PACK, Q], F32, name="hid_raw")
@@ -76,7 +77,6 @@ def tile_attend_adaptivesoftmax_kernel(tc, hid, head, tl, htail, tail_words, tai
         nc.sync.dma_start(out=tl_sb[:], in_=tl)
         nc.sync.dma_start(out=words[0][:].bitcast(I32), in_=tail_words[0].bitcast(I32))
         nc.sync.dma_start(cluster_list[:], offs2)
-        nc.sync.dma_start(out=words[1][:].bitcast(I32), in_=tail_words[1].bitcast(I32))
 
         steps = sb.tile([P, NODES], F32, name="steps")
         nc.gpsimd.iota(steps[:], [[1, NODES]], base=0, channel_multiplier=0, allow_small_or_imprecise_dtypes=True)
@@ -90,15 +90,24 @@ def tile_attend_adaptivesoftmax_kernel(tc, hid, head, tl, htail, tail_words, tai
 
         picked_scales = sb.tile([P, I], U8, name="picked_scales", align_bytes=64)
         nc.vector.tensor_copy(picked_scales[:], scale_rows[:].indirect(word_list[:]))
-        for quad in (0, 2, 1, 3):
+
+        def move_rows(quad, h):
             first = 96 + 8 * quad
             nc.sync.dma_start(
-                out=tail_planes[32 * quad : 32 * quad + 4, :].bitcast(I32),
-                in_=picked_scales[first : first + 8, :].bitcast(I32),
+                out=tail_planes[32 * quad : 32 * quad + 4, h * PASSES * HALF : (h + 1) * PASSES * HALF].bitcast(I32),
+                in_=picked_scales[first : first + 8, h * HALF : (h + 1) * HALF].bitcast(I32),
             )
 
-        htail_raw.append(sb.tile([P, PACK, Q], F32, name="htail_raw1", tag="raw_then_b1", align_bytes=64))
+        move_rows(0, 0)
+        move_rows(2, 0)
+        words.append(shared.tile([P, T], U16, name="words1", offset=0, align_bytes=64))
+        nc.sync.dma_start(out=words[1][:].bitcast(I32), in_=tail_words[1].bitcast(I32))
+        htail_raw.append(shared.tile([P, PACK, Q], F32, name="htail_raw1", tag="raw_then_b1", offset=8192, align_bytes=64))
         nc.sync.dma_start(out=htail_raw[1][:], in_=htail_rows[1])
+        move_rows(1, 0)
+        move_rows(3, 0)
+        for quad in (0, 2, 1, 3):
+            move_rows(quad, 1)
 
         half = U // 2
         head_g = [sb.tile([P, half, PACK], BF16, name=f"head_g{h}", align_bytes=64) for h in range(2)]
@@ -161,7 +170,10 @@ def tile_attend_adaptivesoftmax_kernel(tc, hid, head, tl, htail, tail_words, tai
         picked_b = {}
 
         def look_up(first, last, tag):
-            tile = sb.tile([P, last - first], F32, name=f"picked_b{first}", tag=tag, align_bytes=64)
+            if tag == "raw_then_b1":
+                tile = shared.tile([P, last - first], F32, name=f"picked_b{first}", tag=tag, offset=8192, align_bytes=64)
+            else:
+                tile = sb.tile([P, last - first], F32, name=f"picked_b{first}", tag=tag, align_bytes=64)
             nc.scalar.activation(out=tile[:], in_=b[:].indirect(cluster_list[:, first // 16 : last // 16]), func=ACT.Copy)
             for column in range(first, last, 128):
                 picked_b[column] = (tile, first)
@@ -190,7 +202,7 @@ def tile_attend_adaptivesoftmax_kernel(tc, hid, head, tl, htail, tail_words, tai
                 for g, (first, last) in enumerate(GROUPS):
                     if first // HALF == h:
                         cols = slice(first - h * HALF, last - h * HALF)
-                        plane = z * I + h * HALF
+                        plane = (h * PASSES + z) * HALF
                         nc.tensor.matmul_mx(
                             out=r_bank[g][:],
                             lhsT=htail_codes[z][:].bitcast(FP8X4),

@@ -24,7 +24,7 @@ HALF = I // 2
 LIST_COLS = I // 16
 NODES = 96
 NODE_STEP = math.exp(-1.0)
-FIRST_NODE = -32.0
+FIRST_NODE = -86
 
 
 def interleave(copy, grouped, raw):
@@ -40,8 +40,8 @@ def quantise(nc, codes, scales, grouped):
 
 VECTOR_CASTS = 320
 LOOK_UP = 256
-GROUPS = ((0, 256), (256, 512), (512, 640), (640, 768), (768, 896), (896, 1024))
-STORES = ((256, 512), (0, 256), (512, 768), (768, 896), (896, 1024))
+GROUPS = ((0, 128), (128, 256), (256, 512), (512, 640), (640, 768), (768, 896), (896, 1024))
+STORES = ((0, 128), (256, 512), (128, 256), (512, 768), (768, 896), (896, 1024))
 
 
 def tile_attend_adaptivesoftmax_kernel(tc, hid, head, tl, htail, tail_words, tail_scales, offs, offs2, out):
@@ -53,61 +53,53 @@ def tile_attend_adaptivesoftmax_kernel(tc, hid, head, tl, htail, tail_words, tai
 
         word_list = sb.tile([P, LIST_COLS], U16, name="word_list")
         cluster_list = sb.tile([P, LIST_COLS], U16, name="cluster_list")
-        scale_rows = shared.tile([P, T], U8, name="scale_rows", offset=6144, align_bytes=64)
+        scale_rows = sb.tile([P, T], U8, name="scale_rows", align_bytes=64)
         words = [sb.tile([P, T], U16, name="words0", align_bytes=64)]
         htail_raw = [sb.tile([P, PACK, Q], F32, name=f"htail_raw{z}", tag=f"raw_then_b{z}", align_bytes=64) for z in range(1)]
-        head_raw = sb.tile([P, PACK, U], F32, name="head_raw")
-        hid_raw = sb.tile([P, PACK, Q], F32, name="hid_raw")
+        head_raw = shared.tile([P, PACK, U], F32, name="head_raw", offset=0, align_bytes=64)
+        hid_raw = sb.tile([P, PACK, Q], F32, name="hid_raw", tag="hid_then_planes", align_bytes=64)
         tl_sb = sb.tile([P, U], F32, name="tl_sb")
         b = sb.tile([P, U], F32, name="b")
-        tail_planes = sb.tile([P, PASSES * I], U8, name="tail_planes", align_bytes=64)
+        tail_planes = []
 
         nc.vector.memset(scale_rows[0:96, :].bitcast(I32), 0)
         nc.sync.dma_start(
             out=scale_rows[96:P, :].bitcast(I32),
             in_=tail_scales.bitcast(I32).rearrange("z f t -> f z t"),
         )
-        nc.vector.memset(tail_planes[:].bitcast(I32), 0)
 
         nc.sync.dma_start(word_list[:], offs)
+        nc.sync.dma_start(cluster_list[:], offs2)
         nc.sync.dma_start(out=hid_raw[:], in_=hid.rearrange("(p t) q -> p t q", t=PACK))
         nc.sync.dma_start(out=head_raw[:], in_=head.rearrange("(p t) u -> p t u", t=PACK))
         htail_rows = htail.rearrange("(z p t) q -> z p t q", p=P, t=PACK)
         nc.sync.dma_start(out=htail_raw[0][:], in_=htail_rows[0])
         nc.sync.dma_start(out=tl_sb[:], in_=tl)
         nc.sync.dma_start(out=words[0][:].bitcast(I32), in_=tail_words[0].bitcast(I32))
-        nc.sync.dma_start(cluster_list[:], offs2)
 
         steps = sb.tile([P, NODES], F32, name="steps")
-        nc.gpsimd.iota(steps[:], [[1, NODES]], base=0, channel_multiplier=0, allow_small_or_imprecise_dtypes=True)
+        nc.gpsimd.iota(steps[:], [[1, NODES]], base=FIRST_NODE, channel_multiplier=0, allow_small_or_imprecise_dtypes=True)
         nodes = sb.tile([P, NODES], F32, name="nodes")
-        nc.scalar.activation(out=nodes[:], in_=steps[:], func=ACT.Exp, scale=NODE_STEP, bias=FIRST_NODE)
+        nc.scalar.activation(out=nodes[:], in_=steps[:], func=ACT.Exp, scale=NODE_STEP)
         neg_nodes = sb.tile([P, NODES], F32, name="neg_nodes")
         nc.scalar.activation(out=neg_nodes[:], in_=nodes[:], func=ACT.Copy, scale=-1.0)
         terms = sb.tile([P, NODES], F32, name="terms")
         sum_at_one = sb.tile([P, 1], F32, name="sum_at_one")
         nc.scalar.activation(out=terms[:], in_=neg_nodes[:], func=ACT.Exp, bias=-1.0, accum_out=sum_at_one[:])
 
-        picked_scales = sb.tile([P, I], U8, name="picked_scales", align_bytes=64)
-        nc.vector.tensor_copy(picked_scales[:], scale_rows[:].indirect(word_list[:]))
+        picked_scales = [None, None]
 
-        def move_rows(quad, h):
-            first = 96 + 8 * quad
-            nc.sync.dma_start(
-                out=tail_planes[32 * quad : 32 * quad + 4, h * PASSES * HALF : (h + 1) * PASSES * HALF].bitcast(I32),
-                in_=picked_scales[first : first + 8, h * HALF : (h + 1) * HALF].bitcast(I32),
-            )
+        def move_rows(queue, h):
+            for quad in (0, 2, 1, 3):
+                first = 96 + 8 * quad
+                queue.dma_start(
+                    out=tail_planes[h][32 * quad : 32 * quad + 4, :].bitcast(I32),
+                    in_=picked_scales[h][first : first + 8, :].bitcast(I32),
+                )
 
-        move_rows(0, 0)
-        move_rows(2, 0)
-        words.append(shared.tile([P, T], U16, name="words1", offset=0, align_bytes=64))
-        nc.sync.dma_start(out=words[1][:].bitcast(I32), in_=tail_words[1].bitcast(I32))
-        htail_raw.append(shared.tile([P, PACK, Q], F32, name="htail_raw1", tag="raw_then_b1", offset=8192, align_bytes=64))
-        nc.sync.dma_start(out=htail_raw[1][:], in_=htail_rows[1])
-        move_rows(1, 0)
-        move_rows(3, 0)
-        for quad in (0, 2, 1, 3):
-            move_rows(quad, 1)
+        for h in range(2):
+            picked_scales[h] = sb.tile([P, HALF], U8, name=f"picked_scales{h}", align_bytes=64)
+            nc.vector.tensor_copy(picked_scales[h][:], scale_rows[:].indirect(word_list[:, h * HALF // 16 : (h + 1) * HALF // 16]))
 
         half = U // 2
         head_g = [sb.tile([P, half, PACK], BF16, name=f"head_g{h}", align_bytes=64) for h in range(2)]
@@ -120,8 +112,15 @@ def tile_attend_adaptivesoftmax_kernel(tc, hid, head, tl, htail, tail_words, tai
         interleave(nc.vector.tensor_copy, head_g[0][:], head_raw[:, :, 0:half])
         interleave(nc.vector.tensor_copy, head_g[1][:, 0 : VECTOR_CASTS - half, :], head_raw[:, :, half:VECTOR_CASTS])
         interleave(nc.scalar.copy, head_g[1][:, VECTOR_CASTS - half : half, :], head_raw[:, :, VECTOR_CASTS:U])
+        tail_planes.append(sb.tile([P, PASSES * HALF], U8, name="tail_planes0", tag="hid_then_planes", align_bytes=64))
+        nc.gpsimd.memset(tail_planes[0][:].bitcast(I32), 0)
+        move_rows(nc.scalar, 0)
+        words.append(shared.tile([P, T], U16, name="words1", offset=3072, align_bytes=64))
+        nc.sync.dma_start(out=words[1][:].bitcast(I32), in_=tail_words[1].bitcast(I32))
+        htail_raw.append(shared.tile([P, PACK, Q], F32, name="htail_raw1", tag="raw_then_b1", offset=0, align_bytes=64))
+        nc.sync.dma_start(out=htail_raw[1][:], in_=htail_rows[1])
         quantise(nc, hid_codes[:], hid_plane[:], hid_g[:])
-        a = [ps.tile([P, half], F32, name=f"a{h}") for h in range(2)]
+        a = [ps.tile([P, half], F32, name=f"a{h}", tag=f"bank{h}") for h in range(2)]
         for h in range(2):
             us = slice(h * half, (h + 1) * half)
             quantise(nc, head_codes[:, us], head_plane[:, us], head_g[h][:])
@@ -145,6 +144,9 @@ def tile_attend_adaptivesoftmax_kernel(tc, hid, head, tl, htail, tail_words, tai
         )
         htail_codes[0] = sb.tile([P, Q], U32, name="htail_codes0", tag="hid_then_htail", align_bytes=64)
         quantise(nc, htail_codes[0][:], htail_plane[0][:], early_g[:])
+        tail_planes.append(shared.tile([P, PASSES * HALF], U8, name="tail_planes1", offset=2048, align_bytes=64))
+        nc.vector.memset(tail_planes[1][:].bitcast(I32), 0)
+        move_rows(nc.sync, 1)
         tl_less_a = sb.tile([P, U], F32, name="tl_less_a")
         nc.gpsimd.tensor_tensor(out=tl_less_a[:], in0=neg_a[:], in1=tl_sb[:], op=ALU.add)
         exps = sb.tile([P, U], F32, name="exps")
@@ -171,7 +173,7 @@ def tile_attend_adaptivesoftmax_kernel(tc, hid, head, tl, htail, tail_words, tai
 
         def look_up(first, last, tag):
             if tag == "raw_then_b1":
-                tile = shared.tile([P, last - first], F32, name=f"picked_b{first}", tag=tag, offset=8192, align_bytes=64)
+                tile = shared.tile([P, last - first], F32, name=f"picked_b{first}", tag=tag, offset=0, align_bytes=64)
             else:
                 tile = sb.tile([P, last - first], F32, name=f"picked_b{first}", tag=tag, align_bytes=64)
             nc.scalar.activation(out=tile[:], in_=b[:].indirect(cluster_list[:, first // 16 : last // 16]), func=ACT.Copy)
@@ -183,7 +185,6 @@ def tile_attend_adaptivesoftmax_kernel(tc, hid, head, tl, htail, tail_words, tai
             return tile[:, first - start : last - start]
 
         look_up(0, 256, "first_b")
-        look_up(640, 768, "second_b")
         nc.gpsimd.tensor_scalar(
             out=late_g[:, 0 : Q // 2, :], in0=htail_raw[1][:, :, 0 : Q // 2].rearrange("p t c -> p c t"),
             scalar1=1.0, scalar2=0.0, op0=ALU.mult, op1=ALU.add,
@@ -196,30 +197,31 @@ def tile_attend_adaptivesoftmax_kernel(tc, hid, head, tl, htail, tail_words, tai
 
         look_up(256, 640, "raw_then_b1")
 
-        r_bank = [ps.tile([P, last - first], F32, name=f"r_bank{g}") for g, (first, last) in enumerate(GROUPS)]
+        r_bank = [ps.tile([P, last - first], F32, name=f"r_bank{g}", tag=f"bank{g + 1}") for g, (first, last) in enumerate(GROUPS)]
         for h in range(2):
             for z in range(PASSES):
                 for g, (first, last) in enumerate(GROUPS):
                     if first // HALF == h:
                         cols = slice(first - h * HALF, last - h * HALF)
-                        plane = (h * PASSES + z) * HALF
+                        plane = z * HALF
                         nc.tensor.matmul_mx(
                             out=r_bank[g][:],
                             lhsT=htail_codes[z][:].bitcast(FP8X4),
                             lhsT_scale=htail_plane[z][:],
                             rhs=picked[z][h][:, cols].bitcast(FP4X4),
-                            rhs_scale=tail_planes[:, plane + cols.start : plane + cols.stop],
+                            rhs_scale=tail_planes[h][:, plane + cols.start : plane + cols.stop],
                             start=(z == 0),
                             stop=(z == PASSES - 1),
                         )
 
         result = sb.tile([P, I], F32, name="result")
-        first, last = GROUPS[0]
-        r = sb.tile([P, last - first], F32, name="r")
-        nc.scalar.copy(out=r[:], in_=r_bank[0][:])
-        nc.gpsimd.tensor_tensor(out=result[:, first:last], in0=r[:], in1=b_columns(first, last), op=ALU.add)
-        look_up(768, 1024, "words_then_b")
-        for g in range(1, len(GROUPS)):
+        r = sb.tile([P, 256], F32, name="r")
+        for g in range(2):
+            first, last = GROUPS[g]
+            nc.scalar.copy(out=r[:, first:last], in_=r_bank[g][:])
+            nc.gpsimd.tensor_tensor(out=result[:, first:last], in0=r[:, first:last], in1=b_columns(first, last), op=ALU.add)
+        look_up(640, 1024, "words_then_b")
+        for g in range(2, len(GROUPS)):
             first, last = GROUPS[g]
             nc.vector.tensor_tensor(result[:, first:last], r_bank[g][:], b_columns(first, last), ALU.add)
         for first, last in STORES:

@@ -54,7 +54,7 @@ def tile_attend_adaptivesoftmax_kernel(tc, hid, head, tl, htail, tail_words, tai
         word_list = sb.tile([P, LIST_COLS], U16, name="word_list")
         cluster_list = sb.tile([P, LIST_COLS], U16, name="cluster_list")
         scale_rows = sb.tile([P, T], U8, name="scale_rows", align_bytes=64)
-        words = [sb.tile([P, T], U16, name="words0", align_bytes=64)]
+        words = [sb.tile([P, T], U16, name=f"words{z}", align_bytes=64) for z in range(PASSES)]
         htail_raw = [sb.tile([P, PACK, Q], F32, name=f"htail_raw{z}", tag=f"raw_then_b{z}", align_bytes=64) for z in range(1)]
         head_raw = shared.tile([P, PACK, U], F32, name="head_raw", offset=0, align_bytes=64)
         hid_raw = sb.tile([P, PACK, Q], F32, name="hid_raw", tag="hid_then_planes", align_bytes=64)
@@ -75,7 +75,8 @@ def tile_attend_adaptivesoftmax_kernel(tc, hid, head, tl, htail, tail_words, tai
         htail_rows = htail.rearrange("(z p t) q -> z p t q", p=P, t=PACK)
         nc.sync.dma_start(out=htail_raw[0][:], in_=htail_rows[0])
         nc.sync.dma_start(out=tl_sb[:], in_=tl)
-        nc.sync.dma_start(out=words[0][:].bitcast(I32), in_=tail_words[0].bitcast(I32))
+        for z in range(PASSES):
+            nc.sync.dma_start(out=words[z][:].bitcast(I32), in_=tail_words[z].bitcast(I32))
 
         steps = sb.tile([P, NODES], F32, name="steps")
         nc.gpsimd.iota(steps[:], [[1, NODES]], base=FIRST_NODE, channel_multiplier=0, allow_small_or_imprecise_dtypes=True)
@@ -115,8 +116,6 @@ def tile_attend_adaptivesoftmax_kernel(tc, hid, head, tl, htail, tail_words, tai
         tail_planes.append(sb.tile([P, PASSES * HALF], U8, name="tail_planes0", tag="hid_then_planes", align_bytes=64))
         nc.gpsimd.memset(tail_planes[0][:].bitcast(I32), 0)
         move_rows(nc.scalar, 0)
-        words.append(shared.tile([P, T], U16, name="words1", offset=3072, align_bytes=64))
-        nc.sync.dma_start(out=words[1][:].bitcast(I32), in_=tail_words[1].bitcast(I32))
         htail_raw.append(shared.tile([P, PACK, Q], F32, name="htail_raw1", tag="raw_then_b1", offset=0, align_bytes=64))
         nc.sync.dma_start(out=htail_raw[1][:], in_=htail_rows[1])
         quantise(nc, hid_codes[:], hid_plane[:], hid_g[:])

@@ -39,6 +39,7 @@ def quantise(nc, codes, scales, grouped):
 
 
 VECTOR_CASTS = 320
+GPSIMD_CASTS = 40
 LOOK_UP = 256
 GROUPS = ((0, 128), (128, 256), (256, 512), (512, 640), (640, 768), (768, 896), (896, 1024))
 STORES = ((0, 128), (256, 512), (128, 256), (512, 768), (768, 896), (896, 1024))
@@ -170,12 +171,15 @@ def tile_attend_adaptivesoftmax_kernel(tc, hid, head, tl, htail, tail_words, tai
         late_g = sb.tile([P, Q, PACK], BF16, name="late_g", tag="cast_then_words", align_bytes=64)
         picked_b = {}
 
-        def look_up(first, last, tag):
+        def look_up(first, last, tag, cuts=()):
             if tag == "raw_then_b1":
                 tile = shared.tile([P, last - first], F32, name=f"picked_b{first}", tag=tag, offset=0, align_bytes=64)
             else:
                 tile = sb.tile([P, last - first], F32, name=f"picked_b{first}", tag=tag, align_bytes=64)
-            nc.scalar.activation(out=tile[:], in_=b[:].indirect(cluster_list[:, first // 16 : last // 16]), func=ACT.Copy)
+            for start, stop in zip((first, *cuts), (*cuts, last)):
+                nc.scalar.activation(
+                    out=tile[:, start - first : stop - first], in_=b[:].indirect(cluster_list[:, start // 16 : stop // 16]), func=ACT.Copy
+                )
             for column in range(first, last, 128):
                 picked_b[column] = (tile, first)
 
@@ -183,18 +187,18 @@ def tile_attend_adaptivesoftmax_kernel(tc, hid, head, tl, htail, tail_words, tai
             tile, start = picked_b[first]
             return tile[:, first - start : last - start]
 
-        look_up(0, 256, "first_b")
+        look_up(0, 128, "first_b")
         nc.gpsimd.tensor_scalar(
-            out=late_g[:, 0 : Q // 2, :], in0=htail_raw[1][:, :, 0 : Q // 2].rearrange("p t c -> p c t"),
+            out=late_g[:, 0:GPSIMD_CASTS, :], in0=htail_raw[1][:, :, 0:GPSIMD_CASTS].rearrange("p t c -> p c t"),
             scalar1=1.0, scalar2=0.0, op0=ALU.mult, op1=ALU.add,
         )
-        interleave(nc.scalar.copy, late_g[:, Q // 2 : Q, :], htail_raw[1][:, :, Q // 2 : Q])
+        interleave(nc.scalar.copy, late_g[:, GPSIMD_CASTS:Q, :], htail_raw[1][:, :, GPSIMD_CASTS:Q])
         quantise(nc, htail_codes[1][:], htail_plane[1][:], late_g[:])
         late = sb.tile([P, HALF], U16, name="late", tag="cast_then_words", align_bytes=64)
         nc.vector.tensor_copy(late[:], words[1][:].indirect(word_list[:, HALF // 16 : I // 16]))
         picked = [[first_pass[:, 0:HALF], first_pass[:, HALF:I]], [early[:], late[:]]]
 
-        look_up(256, 640, "raw_then_b1")
+        look_up(128, 512, "raw_then_b1")
 
         r_bank = [ps.tile([P, last - first], F32, name=f"r_bank{g}", tag=f"bank{g + 1}") for g, (first, last) in enumerate(GROUPS)]
         for h in range(2):
@@ -219,7 +223,7 @@ def tile_attend_adaptivesoftmax_kernel(tc, hid, head, tl, htail, tail_words, tai
             first, last = GROUPS[g]
             nc.scalar.copy(out=r[:, first:last], in_=r_bank[g][:])
             nc.gpsimd.tensor_tensor(out=result[:, first:last], in0=r[:, first:last], in1=b_columns(first, last), op=ALU.add)
-        look_up(640, 1024, "words_then_b")
+        look_up(512, 1024, "words_then_b", cuts=(768, 896))
         for g in range(2, len(GROUPS)):
             first, last = GROUPS[g]
             nc.vector.tensor_tensor(result[:, first:last], r_bank[g][:], b_columns(first, last), ALU.add)

import math
from contextlib import ExitStack

import concourse.mybir as mybir

D, K, T, I, U, Q = 512, 1024, 4096, 1024, 512, 128
FLOPS = 2 * Q * D * U + 2 * Q * K * I

F32 = mybir.dt.float32
BF16 = mybir.dt.bfloat16
I32 = mybir.dt.int32
U32 = mybir.dt.uint32
U16 = mybir.dt.uint16
U8 = mybir.dt.uint8
FP8X4 = mybir.dt.float8_e4m3fn_x4
FP4X4 = mybir.dt.float4_e2m1fn_x4
ALU = mybir.AluOpType
ACT = mybir.ActivationFunctionType

P = 128
PACK = 4
PASSES = K // (P * PACK)
HALF = I // 2
LIST_COLS = I // 16
NODES = 96
NODE_STEP = math.exp(-1.0)
FIRST_NODE = -86


def interleave(copy, grouped, raw):
    copy(
        out=grouped.rearrange("p (c i) t -> p c t i", i=4),
        in_=raw.rearrange("p t (c i) -> p c t i", i=4),
    )


def quantise(nc, codes, scales, grouped):
    nc.vector.quantize_mx(out=codes.bitcast(FP8X4), scales=scales, in_=grouped.rearrange("p c t -> p (c t)"))


VECTOR_CASTS = 320
GPSIMD_CASTS = 40
LOOK_UP = 256
GROUPS = ((0, 128), (128, 256), (256, 512), (512, 640), (640, 768), (768, 896), (896, 1024))
STORES = ((0, 128), (256, 512), (128, 256), (512, 768), (768, 896), (896, 1024))


def tile_attend_adaptivesoftmax_kernel(tc, hid, head, tl, htail, tail_words, tail_scales, offs, offs2, out):
    nc = tc.nc
    with ExitStack() as ctx:
        sb = ctx.enter_context(tc.tile_pool(name="sb", bufs=1))
        shared = ctx.enter_context(tc.tile_pool(name="shared", bufs=1))
        ps = ctx.enter_context(tc.psum_pool(name="ps", bufs=1))

        word_list = sb.tile([P, LIST_COLS], U16, name="word_list")
        cluster_list = sb.tile([P, LIST_COLS], U16, name="cluster_list")
        scale_rows = sb.tile([P, T], U8, name="scale_rows", align_bytes=64)
        words = [sb.tile([P, T], U16, name=f"words{z}", align_bytes=64) for z in range(PASSES)]
        htail_raw = [sb.tile([P, PACK, Q], F32, name=f"htail_raw{z}", tag=f"raw_then_b{z}", align_bytes=64) for z in range(1)]
        head_raw = shared.tile([P, PACK, U], F32, name="head_raw", offset=0, align_bytes=64)
        hid_raw = sb.tile([P, PACK, Q], F32, name="hid_raw", tag="hid_then_planes", align_bytes=64)
        tl_sb = sb.tile([P, U], F32, name="tl_sb")
        b = sb.tile([P, U], F32, name="b")
        tail_planes = []

        nc.vector.memset(scale_rows[0:96, :].bitcast(I32), 0)
        nc.sync.dma_start(
            out=scale_rows[96:P, :].bitcast(I32),
            in_=tail_scales.bitcast(I32).rearrange("z f t -> f z t"),
        )

        nc.sync.dma_start(word_list[:], offs)
        nc.sync.dma_start(cluster_list[:], offs2)
        nc.sync.dma_start(out=hid_raw[:], in_=hid.rearrange("(p t) q -> p t q", t=PACK))
        nc.sync.dma_start(out=head_raw[:], in_=head.rearrange("(p t) u -> p t u", t=PACK))
        htail_rows = htail.rearrange("(z p t) q -> z p t q", p=P, t=PACK)
        nc.sync.dma_start(out=htail_raw[0][:], in_=htail_rows[0])
        nc.sync.dma_start(out=tl_sb[:], in_=tl)
        for z in range(PASSES):
            nc.sync.dma_start(out=words[z][:].bitcast(I32), in_=tail_words[z].bitcast(I32))

        steps = sb.tile([P, NODES], F32, name="steps")
        nc.gpsimd.iota(steps[:], [[1, NODES]], base=FIRST_NODE, channel_multiplier=0, allow_small_or_imprecise_dtypes=True)
        nodes = sb.tile([P, NODES], F32, name="nodes")
        nc.scalar.activation(out=nodes[:], in_=steps[:], func=ACT.Exp, scale=NODE_STEP)
        neg_nodes = sb.tile([P, NODES], F32, name="neg_nodes")
        nc.scalar.activation(out=neg_nodes[:], in_=nodes[:], func=ACT.Copy, scale=-1.0)
        terms = sb.tile([P, NODES], F32, name="terms")
        sum_at_one = sb.tile([P, 1], F32, name="sum_at_one")
        nc.scalar.activation(out=terms[:], in_=neg_nodes[:], func=ACT.Exp, bias=-1.0, accum_out=sum_at_one[:])

        picked_scales = [None, None]

        def move_rows(queue, h):
            for quad in (0, 2, 1, 3):
                first = 96 + 8 * quad
                queue.dma_start(
                    out=tail_planes[h][32 * quad : 32 * quad + 4, :].bitcast(I32),
                    in_=picked_scales[h][first : first + 8, :].bitcast(I32),
                )

        for h in range(2):
            picked_scales[h] = sb.tile([P, HALF], U8, name=f"picked_scales{h}", align_bytes=64)
            nc.vector.tensor_copy(picked_scales[h][:], scale_rows[:].indirect(word_list[:, h * HALF // 16 : (h + 1) * HALF // 16]))

        half = U // 2
        head_g = [sb.tile([P, half, PACK], BF16, name=f"head_g{h}", align_bytes=64) for h in range(2)]
        hid_g = sb.tile([P, Q, PACK], BF16, name="hid_g", align_bytes=64)
        head_codes = sb.tile([P, U], U32, name="head_codes", tag="codes_then_words", align_bytes=64)
        head_plane = sb.tile([P, U], U8, name="head_plane", align_bytes=64)
        hid_codes = sb.tile([P, Q], U32, name="hid_codes", tag="hid_then_htail", align_bytes=64)
        hid_plane = sb.tile([P, Q], U8, name="hid_plane", align_bytes=64)
        interleave(nc.scalar.copy, hid_g[:], hid_raw[:])
        interleave(nc.vector.tensor_copy, head_g[0][:], head_raw[:, :, 0:half])
        interleave(nc.vector.tensor_copy, head_g[1][:, 0 : VECTOR_CASTS - half, :], head_raw[:, :, half:VECTOR_CASTS])
        interleave(nc.scalar.copy, head_g[1][:, VECTOR_CASTS - half : half, :], head_raw[:, :, VECTOR_CASTS:U])
        tail_planes.append(sb.tile([P, PASSES * HALF], U8, name="tail_planes0", tag="hid_then_planes", align_bytes=64))
        nc.gpsimd.memset(tail_planes[0][:].bitcast(I32), 0)
        move_rows(nc.scalar, 0)
        htail_raw.append(shared.tile([P, PACK, Q], F32, name="htail_raw1", tag="raw_then_b1", offset=0, align_bytes=64))
        nc.sync.dma_start(out=htail_raw[1][:], in_=htail_rows[1])
        quantise(nc, hid_codes[:], hid_plane[:], hid_g[:])
        a = [ps.tile([P, half], F32, name=f"a{h}", tag=f"bank{h}") for h in range(2)]
        for h in range(2):
            us = slice(h * half, (h + 1) * half)
            quantise(nc, head_codes[:, us], head_plane[:, us], head_g[h][:])
            nc.tensor.matmul_mx(
                out=a[h][:], lhsT=hid_codes[:].bitcast(FP8X4), lhsT_scale=hid_plane[:],
                rhs=head_codes[:, us].bitcast(FP8X4), rhs_scale=head_plane[:, us], start=True, stop=True,
            )
        htail_codes = [None, sb.tile([P, Q], U32, name="htail_codes1", align_bytes=64)]
        htail_plane = [sb.tile([P, Q], U8, name=f"htail_plane{z}", align_bytes=64) for z in range(PASSES)]
        early_g = sb.tile([P, Q, PACK], BF16, name="early_g", align_bytes=64)
        interleave(nc.scalar.copy, early_g[:], htail_raw[0][:])

        neg_a = sb.tile([P, U], F32, name="neg_a")
        neg_half_max = sb.tile([P, 1], F32, name="neg_half_max")
        neg_max = sb.tile([P, 1], F32, name="neg_max")
        nc.vector.tensor_scalar(
            out=neg_a[:, 0:half], in0=a[0][:], scalar1=-1.0, scalar2=None, op0=ALU.mult, op1=ALU.min, accum_out=neg_half_max[:]
        )
        nc.vector.tensor_scalar(
            out=neg_a[:, half:U], in0=a[1][:], scalar1=-1.0, scalar2=neg_half_max[:], op0=ALU.mult, op1=ALU.min, accum_out=neg_max[:]
        )
        htail_codes[0] = sb.tile([P, Q], U32, name="htail_codes0", tag="hid_then_htail", align_bytes=64)
        quantise(nc, htail_codes[0][:], htail_plane[0][:], early_g[:])
        tail_planes.append(shared.tile([P, PASSES * HALF], U8, name="tail_planes1", offset=2048, align_bytes=64))
        nc.vector.memset(tail_planes[1][:].bitcast(I32), 0)
        move_rows(nc.sync, 1)
        tl_less_a = sb.tile([P, U], F32, name="tl_less_a")
        nc.gpsimd.tensor_tensor(out=tl_less_a[:], in0=neg_a[:], in1=tl_sb[:], op=ALU.add)
        exps = sb.tile([P, U], F32, name="exps")
        row_sum = sb.tile([P, 1], F32, name="row_sum")
        nc.scalar.activation(out=exps[:], in_=neg_a[:], func=ACT.Exp, scale=-1.0, bias=neg_max[:], accum_out=row_sum[:])
        base = sb.tile([P, 1], F32, name="base")
        nc.scalar.activation(out=base[:], in_=sum_at_one[:], func=ACT.Identity, scale=-1.0, bias=neg_max[:])
        row_terms = sb.tile([P, NODES], F32, name="row_terms")
        sum_at_row = sb.tile([P, 1], F32, name="sum_at_row")
        nc.scalar.activation(out=row_terms[:], in_=neg_nodes[:], func=ACT.Exp, scale=row_sum[:], bias=-1.0, accum_out=sum_at_row[:])
        shift = sb.tile([P, 1], F32, name="shift")
        nc.scalar.activation(out=shift[:], in_=sum_at_row[:], func=ACT.Identity, bias=base[:])
        nc.gpsimd.tensor_scalar(
            out=b[:, 0:half], in0=tl_less_a[:, 0:half], scalar1=-1.0, scalar2=shift[:], op0=ALU.mult, op1=ALU.add
        )
        nc.scalar.activation(out=b[:, half:U], in_=tl_less_a[:, half:U], func=ACT.Identity, scale=-1.0, bias=shift[:])

        first_pass = sb.tile([P, I], U16, name="first_pass", tag="codes_then_words", align_bytes=64)
        nc.vector.tensor_copy(first_pass[:], words[0][:].indirect(word_list[:]))
        early = sb.tile([P, HALF], U16, name="early", tag="words_then_b", align_bytes=64)
        nc.vector.tensor_copy(early[:], words[1][:].indirect(word_list[:, 0 : HALF // 16]))
        late_g = sb.tile([P, Q, PACK], BF16, name="late_g", tag="cast_then_words", align_bytes=64)
        picked_b = {}

        def look_up(first, last, tag, cuts=()):
            if tag == "raw_then_b1":
                tile = shared.tile([P, last - first], F32, name=f"picked_b{first}", tag=tag, offset=0, align_bytes=64)
            else:
                tile = sb.tile([P, last - first], F32, name=f"picked_b{first}", tag=tag, align_bytes=64)
            for start, stop in zip((first, *cuts), (*cuts, last)):
                nc.scalar.activation(
                    out=tile[:, start - first : stop - first], in_=b[:].indirect(cluster_list[:, start // 16 : stop // 16]), func=ACT.Copy
                )
            for column in range(first, last, 128):
                picked_b[column] = (tile, first)

        def b_columns(first, last):
            tile, start = picked_b[first]
            return tile[:, first - start : last - start]

        look_up(0, 128, "first_b")
        nc.gpsimd.tensor_scalar(
            out=late_g[:, 0:GPSIMD_CASTS, :], in0=htail_raw[1][:, :, 0:GPSIMD_CASTS].rearrange("p t c -> p c t"),
            scalar1=1.0, scalar2=0.0, op0=ALU.mult, op1=ALU.add,
        )
        interleave(nc.scalar.copy, late_g[:, GPSIMD_CASTS:Q, :], htail_raw[1][:, :, GPSIMD_CASTS:Q])
        quantise(nc, htail_codes[1][:], htail_plane[1][:], late_g[:])
        late = sb.tile([P, HALF], U16, name="late", tag="cast_then_words", align_bytes=64)
        nc.vector.tensor_copy(late[:], words[1][:].indirect(word_list[:, HALF // 16 : I // 16]))
        picked = [[first_pass[:, 0:HALF], first_pass[:, HALF:I]], [early[:], late[:]]]

        look_up(128, 512, "raw_then_b1")

        r_bank = [ps.tile([P, last - first], F32, name=f"r_bank{g}", tag=f"bank{g + 1}") for g, (first, last) in enumerate(GROUPS)]
        for h in range(2):
            for z in range(PASSES):
                for g, (first, last) in enumerate(GROUPS):
                    if first // HALF == h:
                        cols = slice(first - h * HALF, last - h * HALF)
                        plane = z * HALF
                        nc.tensor.matmul_mx(
                            out=r_bank[g][:],
                            lhsT=htail_codes[z][:].bitcast(FP8X4),
                            lhsT_scale=htail_plane[z][:],
                            rhs=picked[z][h][:, cols].bitcast(FP4X4),
                            rhs_scale=tail_planes[h][:, plane + cols.start : plane + cols.stop],
                            start=(z == 0),
                            stop=(z == PASSES - 1),
                        )

        result = sb.tile([P, I], F32, name="result")
        r = sb.tile([P, 256], F32, name="r")
        for g in range(2):
            first, last = GROUPS[g]
            nc.scalar.copy(out=r[:, first:last], in_=r_bank[g][:])
            nc.gpsimd.tensor_tensor(out=result[:, first:last], in0=r[:, first:last], in1=b_columns(first, last), op=ALU.add)
        look_up(512, 1024, "words_then_b", cuts=(768, 896))
        for g in range(2, len(GROUPS)):
            first, last = GROUPS[g]
            nc.vector.tensor_tensor(result[:, first:last], r_bank[g][:], b_columns(first, last), ALU.add)
        for first, last in STORES:
            nc.sync.dma_start(out=out[:, first:last], in_=result[:, first:last])
